import numpy as np
import ml_dtypes


def mxq(x, axis, fmt="e4m3"):
    dtype, down = {"e4m3": (ml_dtypes.float8_e4m3fn, 7), "e5m2": (ml_dtypes.float8_e5m2, 14)}[fmt]
    v = np.moveaxis(np.asarray(x, np.float32).astype(ml_dtypes.bfloat16).astype(np.float64), axis, -1)
    blocks = v.reshape(v.shape[:-1] + (-1, 32))
    amax = np.abs(blocks).max(-1, keepdims=True)
    byte = np.maximum(np.where(amax > 0, np.frexp(amax)[1] - 1 + 127, 0) - down, 1)
    scale = np.exp2(byte - 127.0)
    codes = (blocks / scale).astype(np.float32).astype(dtype).astype(np.float64)
    return np.moveaxis((codes * scale).reshape(v.shape), -1, axis)


WIDE = False


def mx_kscale(k):
    if not WIDE:
        return np.ones(k)
    levels = np.array([24, -24, 12, -12, 0])
    if k % 512:
        return np.exp2(np.random.permutation(np.resize(levels, k // 32))).repeat(32)
    a = np.empty((k // 512, 16))
    for p in range(k // 512):
        a[p, :8] = np.random.permutation(np.resize(levels, 8))
        for g in range(8):
            far = levels[np.abs(levels - a[p, g]) >= 10]
            a[p, g + 8] = far[np.random.randint(len(far))]
    return np.exp2(a.ravel()).repeat(32)


def f64(x):
    return np.asarray(x).astype(np.float64)


def striped(idx):
    return np.tile(idx.reshape(-1, 16).T, (8, 1)).astype(np.uint16)


def unstriped(offs):
    return offs[:16].T.reshape(-1).astype(np.int64)


E2M1 = np.array([0.0, 0.5, 1.0, 1.5, 2.0, 3.0, 4.0, 6.0, -0.0, -0.5, -1.0, -1.5, -2.0, -3.0, -4.0, -6.0])


def pack_weight(w, fmt):
    k, n = w.shape
    w = f64(np.asarray(w, np.float32).astype(ml_dtypes.bfloat16)).reshape(k // 32, 32, n)
    amax = np.abs(w).max(1)
    if fmt == "e4m3":
        byte = np.frexp(amax)[1] - 1 + 127 - 7
    else:
        mant, ex = np.frexp(amax / 6.0)
        byte = np.where(mant > 0.5, ex, ex - 1) + 127
    byte = np.clip(np.where(amax > 0, byte, 1), 1, 254)
    scaled = (w * np.exp2(127.0 - byte)[:, None, :]).reshape(k, n).astype(np.float32)
    by_word = np.ascontiguousarray(scaled.reshape(k // 512, 128, 4, n).transpose(0, 1, 3, 2))
    if fmt == "e4m3":
        words = by_word.astype(ml_dtypes.float8_e4m3fn).view(np.uint8)
    else:
        c = by_word.astype(ml_dtypes.float4_e2m1fn).view(np.uint8) & 0xF
        words = (c[..., 0::2] | (c[..., 1::2] << 4)).reshape(k // 512, 128, 2 * n)
    return np.ascontiguousarray(words), np.ascontiguousarray(byte.astype(np.uint8).reshape(k // 512, 16, n))


def unpack_weight(words, scales, fmt):
    g, _, n = scales.shape
    words = np.ascontiguousarray(words).reshape(g, 128, n, -1)
    if fmt == "e4m3":
        vals = words.view(ml_dtypes.float8_e4m3fn).astype(np.float64)
    else:
        nib = np.empty((g, 128, n, 4), np.uint8)
        nib[..., 0::2] = words & 0xF
        nib[..., 1::2] = words >> 4
        vals = E2M1[nib]
    vals = vals * np.repeat(np.exp2(scales.astype(np.float64) - 127.0), 8, axis=1)[..., None]
    return vals.transpose(0, 1, 3, 2).reshape(g * 512, n)


def pack_table4(v):
    words, scales = pack_weight(v, "e2m1")
    g, t = words.shape[0] // 2, v.shape[1]
    return np.ascontiguousarray(words.reshape(g, 2, 128, t, 2).transpose(0, 2, 3, 1, 4).reshape(g, 128, t, 4)), scales


def unpack_table4(words, scales):
    g, _, t, _ = words.shape
    return unpack_weight(words.reshape(g, 128, t, 2, 2).transpose(0, 3, 1, 2, 4).reshape(2 * g, 128, 2 * t), scales, "e2m1")


K, L, N, T, J = 1024, 1024, 512, 4096, 512


def setup_inputs():
    n = np.random.standard_normal
    s = mx_kscale(K)[:, None]
    s2 = mx_kscale(L)[:, None]
    p_tab = pack_table4(n((K, T)) * s)
    p_w = pack_weight(n((K, N)) / np.sqrt(K) / s, "e4m3")
    p_wx = pack_weight(n((L, N)) / np.sqrt(L) / s2, "e4m3")
    return {
        "tab_words": p_tab[0],
        "tab_scales": p_tab[1],
        "w_words": p_w[0],
        "w_scales": p_w[1],
        "x": (n((L, J)) * s2).astype(np.float32),
        "wx_words": p_wx[0],
        "wx_scales": p_wx[1],
        "iw0": (np.random.uniform(0.1, 0.6, J)).astype(np.float32),
        "iw1": (np.random.uniform(0.1, 0.6, J)).astype(np.float32),
        "iw2": (np.random.uniform(0.1, 0.6, J)).astype(np.float32),
        "iw3": (np.random.uniform(0.1, 0.6, J)).astype(np.float32),
        "offs": striped(np.concatenate([np.random.permutation(T)[:J] for _ in range(4)])),
    }


def reference(tab_words, tab_scales, w_words, w_scales, x, wx_words, wx_scales, iw0, iw1, iw2, iw3, offs):
    idx = unstriped(offs).reshape(4, J)
    tab_ = unpack_table4(tab_words, tab_scales)[:, idx]
    w_ = unpack_weight(w_words, w_scales, "e4m3")
    a0 = w_.T @ tab_[:, 0]
    a1 = w_.T @ tab_[:, 1]
    a2 = w_.T @ tab_[:, 2]
    a3 = w_.T @ tab_[:, 3]
    x_ = mxq(f64(x), 0, "e4m3")
    wx_ = unpack_weight(wx_words, wx_scales, "e4m3")
    ax = wx_.T @ x_
    return a0 * f64(iw0)[None, :] + a1 * f64(iw1)[None, :] + a2 * f64(iw2)[None, :] + a3 * f64(iw3)[None, :] + ax

@@ -1,0 +1,205 @@
+from contextlib import ExitStack
+
+import concourse.mybir as mybir
+from concourse.masks import make_identity
+
+K, L, N, T, J = 1024, 1024, 512, 4096, 512
+G = 4
+P = 128
+PASSES = 2
+JT = J // P
+NT = N // P
+FLOPS = 2 * N * J * (G * K + L)
+
+F32 = mybir.dt.float32
+BF16 = mybir.dt.bfloat16
+I32 = mybir.dt.int32
+U32 = mybir.dt.uint32
+U16 = mybir.dt.uint16
+U8 = mybir.dt.uint8
+FP8X4 = mybir.dt.float8_e4m3fn_x4
+FP4X4 = mybir.dt.float4_e2m1fn_x4
+MULT = mybir.AluOpType.mult
+ADD = mybir.AluOpType.add
+COPY = mybir.ActivationFunctionType.Copy
+SHIFT = 16
+
+
+def tile_list_interp_none_kernel(
+    tc, tab_words, tab_scales, w_words, w_scales, x, wx_words, wx_scales, iw0, iw1, iw2, iw3, offs, out
+):
+    nc = tc.nc
+    with ExitStack() as ctx:
+        keep = ctx.enter_context(tc.tile_pool(name="keep", bufs=1))
+        accs = ctx.enter_context(tc.psum_pool(name="accs", bufs=6))
+        turns = ctx.enter_context(tc.psum_pool(name="turns", bufs=2))
+
+        offsets = keep.tile([P, G * J // 16], U16, name="offsets")
+        nc.sync.dma_start(offsets[:], offs)
+
+        tab_sc = keep.tile([P, T // 4], I32, name="tab_sc", align_bytes=64)
+        nc.vector.memset(tab_sc[:], 0)
+        iw_rows = keep.tile([P, P], F32, name="iw_rows")
+        nc.gpsimd.memset(iw_rows[:], 0.0)
+        w_sc = keep.tile([P, PASSES, N // 4], I32, name="w_sc", align_bytes=64)
+        nc.vector.memset(w_sc[:], 0)
+        wx_sc = keep.tile([P, PASSES, N // 4], I32, name="wx_sc", align_bytes=64)
+        nc.vector.memset(wx_sc[:], 0)
+        moved = [keep.tile([P, 2 * J // 4], I32, name=f"moved{h}", align_bytes=64) for h in range(2)]
+        for h in range(2):
+            nc.vector.memset(moved[h][:], 0)
+
+        def load_scales(engine, scales, plane):
+            for q in range(4):
+                engine.dma_start(
+                    plane[32 * q : 32 * q + 4, :, :],
+                    scales[:, 4 * q : 4 * q + 4, :].rearrange("a r n -> r a n").bitcast(I32),
+                )
+
+        sc_rows = tab_scales.rearrange("a (q r) t -> r q a t", r=4)
+        for r in range(4):
+            nc.sync.dma_start(tab_sc[r:P:SHIFT, :], sc_rows[r].bitcast(I32))
+        w_c = keep.tile([P, PASSES, N], I32, name="w_c", align_bytes=64)
+        nc.sync.dma_start(w_c[:], w_words.rearrange("a p n i -> p a (n i)").bitcast(I32))
+        tab_w = keep.tile([P, T], I32, name="tab_w", align_bytes=64)
+        nc.sync.dma_start(tab_w[:], tab_words[0].rearrange("p t b -> p (t b)").bitcast(I32))
+        load_scales(nc.sync, w_scales, w_sc)
+        x_raw = [keep.tile([P, 4, J], F32, name=f"x_raw{a}") for a in range(PASSES)]
+        for a in range(PASSES):
+            nc.sync.dma_start(x_raw[a][:], x[512 * a : 512 * (a + 1), :].rearrange("(p i) j -> p i j", i=4))
+        wx_c = keep.tile([P, PASSES, N], I32, name="wx_c", align_bytes=64)
+        nc.sync.dma_start(wx_c[:], wx_words.rearrange("a p n i -> p a (n i)").bitcast(I32))
+
+        for g, iw in enumerate((iw0, iw1, iw2, iw3)):
+            nc.gpsimd.dma_start(iw_rows[JT * g : JT * (g + 1), :], iw.rearrange("(c j) -> c j", j=P))
+        ident = keep.tile([P, P], F32, name="ident")
+        make_identity(nc, ident[:])
+        load_scales(nc.gpsimd, wx_scales, wx_sc)
+
+        iw_ps = turns.tile([P, N], F32, name="turn", tag="turn")
+        nc.tensor.transpose(iw_ps[:, 0:P], iw_rows[:], ident[:])
+        iw_col = keep.tile([P, G * JT], F32, name="iw_col")
+        nc.scalar.copy(iw_col[:], iw_ps[:, 0 : G * JT])
+
+        picked_sc = {}
+        parted = {}
+
+        def gather_scales(h, tag):
+            gs = keep.tile([P, 2 * J], U8, name=f"picked_sc{h}", tag=tag, align_bytes=64)
+            nc.vector.tensor_copy(gs[:], tab_sc[:].bitcast(U8).indirect(offsets[:, 64 * h : 64 * (h + 1)]))
+            nc.scalar.dma_start(moved[h][0 : P - SHIFT, :], gs[SHIFT:P, :].bitcast(I32))
+            picked_sc[h] = gs
+
+        def gather_words(g, tag):
+            gw = keep.tile([P, J], U32, name=f"picked_w{g}", tag=tag, align_bytes=64)
+            nc.vector.tensor_copy(gw[:], tab_w[:].bitcast(U32).indirect(offsets[:, 32 * g : 32 * (g + 1)]))
+            return gw
+
+        def part(g, gw):
+            pt = keep.tile([P, PASSES, 2 * J], U8, name=f"parted{g}", align_bytes=64)
+            src = gw[:].bitcast(U16).rearrange("p (j d) -> p d j", d=PASSES)
+            if g == 0:
+                for a in range(PASSES):
+                    nc.vector.tensor_copy(pt[:, a, :].bitcast(U16), src[:, a, :])
+            else:
+                nc.vector.tensor_copy(pt[:].bitcast(U16), src)
+            parted[g] = pt
+
+        def table_pass(acc, g, jt, a):
+            col = (g % 2) * J + jt * P
+            if a == 0:
+                plane = picked_sc[g // 2][:, col : col + P]
+            else:
+                plane = moved[g // 2][:].bitcast(U8)[:, col : col + P]
+            nc.tensor.matmul_mx(
+                out=acc[:],
+                lhsT=parted[g][:, a, 2 * jt * P : 2 * (jt + 1) * P].bitcast(FP4X4),
+                lhsT_scale=plane,
+                rhs=w_c[:, a, :].bitcast(FP8X4),
+                rhs_scale=w_sc[:, a, :].bitcast(U8),
+                start=(a == 0),
+                stop=(a == PASSES - 1),
+            )
+
+        def weight(g, jt):
+            return iw_col[:, JT * g + jt : JT * g + jt + 1]
+
+        gather_scales(0, "sc0")
+        gather_scales(1, "sc1")
+        part(0, gather_words(0, "w0"))
+        part(1, gather_words(1, "w1"))
+
+        scaled = {}
+        acc0 = [accs.tile([P, N], F32, name="acc", tag="acc") for jt in range(JT)]
+        for a in range(PASSES):
+            for jt in range(JT):
+                table_pass(acc0[jt], 0, jt, a)
+        for jt in range(JT):
+            s = keep.tile([P, N], F32, name=f"scaled0_{jt}")
+            nc.scalar.activation(s[:], acc0[jt][:], COPY, scale=weight(0, jt))
+            scaled[0, jt] = s
+        for jt in range(JT):
+            acc = accs.tile([P, N], F32, name="acc", tag="acc")
+            for a in range(PASSES):
+                table_pass(acc, 1, jt, a)
+            s = keep.tile([P, N], F32, name=f"scaled1_{jt}")
+            nc.scalar.activation(s[:], acc[:], COPY, scale=weight(1, jt))
+            scaled[1, jt] = s
+
+        part(2, gather_words(2, "w2"))
+        part(3, gather_words(3, "w3"))
+
+        x_c = keep.tile([P, PASSES, J], U32, name="x_c", align_bytes=64)
+        x_sc = keep.tile([P, PASSES, J], U8, name="x_sc", align_bytes=64)
+        H = J // 2
+        for a in range(PASSES):
+            for h in range(2):
+                xb = keep.tile([P, H, 4], BF16, name=f"xb{a}{h}", align_bytes=64)
+                nc.scalar.copy(
+                    xb[:].rearrange("p (c i) t -> p c t i", i=4),
+                    x_raw[a][:, :, h * H : (h + 1) * H].rearrange("p t (c i) -> p c t i", i=4),
+                )
+                nc.vector.quantize_mx(
+                    out=x_c[:, a, h * H : (h + 1) * H].bitcast(FP8X4),
+                    scales=x_sc[:, a, h * H : (h + 1) * H],
+                    in_=xb[:].rearrange("p c t -> p (c t)"),
+                )
+
+        out_v = out.rearrange("(t p) j -> p t j", p=P)
+        for jt in range(JT):
+            total = scaled[1, jt]
+            for g in (2, 3):
+                acc = accs.tile([P, N], F32, name="acc", tag="acc")
+                for a in range(PASSES):
+                    table_pass(acc, g, jt, a)
+                nxt = keep.tile([P, N], F32, name=f"sum{g}_{jt}")
+                nc.vector.scalar_tensor_tensor(nxt[:], acc[:], weight(g, jt), total[:], MULT, ADD)
+                total = nxt
+            acc = accs.tile([P, N], F32, name="acc", tag="acc")
+            for a in range(PASSES):
+                nc.tensor.matmul_mx(
+                    out=acc[:],
+                    lhsT=x_c[:, a, jt * P : (jt + 1) * P].bitcast(FP8X4),
+                    lhsT_scale=x_sc[:, a, jt * P : (jt + 1) * P],
+                    rhs=wx_c[:, a, :].bitcast(FP8X4),
+                    rhs_scale=wx_sc[:, a, :].bitcast(U8),
+                    start=(a == 0),
+                    stop=(a == PASSES - 1),
+                )
+            last = keep.tile([P, N], F32, name=f"sumx_{jt}")
+            nc.vector.tensor_tensor(last[:], acc[:], total[:], ADD)
+            turn = turns.tile([P, N], F32, name="turn", tag="turn")
+            terms = (scaled[0, jt], last)
+            for s, term in enumerate(terms):
+                for nt in range(NT):
+                    nc.tensor.matmul(
+                        turn[:, nt * P : (nt + 1) * P],
+                        term[:, nt * P : (nt + 1) * P],
+                        ident[:],
+                        start=(s == 0 and nt == 0),
+                        stop=(s == len(terms) - 1 and nt == NT - 1),
+                        is_transpose=True,
+                    )
+            res = keep.tile([P, NT, P], F32, name=f"res{jt}")
+            nc.scalar.copy(res[:].rearrange("p t j -> p (t j)"), turn[:])
+            nc.sync.dma_start(out_v[:, :, jt * P : (jt + 1) * P], res[:])

@@ -1,7 +1,6 @@
 from contextlib import ExitStack
 
 import concourse.mybir as mybir
-from concourse.masks import make_identity
 
 K, L, N, T, J = 1024, 1024, 512, 4096, 512
 G = 4
@@ -21,6 +20,7 @@ FP8X4 = mybir.dt.float8_e4m3fn_x4
 FP4X4 = mybir.dt.float4_e2m1fn_x4
 MULT = mybir.AluOpType.mult
 ADD = mybir.AluOpType.add
+EQ = mybir.AluOpType.is_equal
 COPY = mybir.ActivationFunctionType.Copy
 SHIFT = 16
 
@@ -31,26 +31,28 @@ def tile_list_interp_none_kernel(
     nc = tc.nc
     with ExitStack() as ctx:
         keep = ctx.enter_context(tc.tile_pool(name="keep", bufs=1))
+        reuse = ctx.enter_context(tc.tile_pool(name="reuse", bufs=1))
+        stage = ctx.enter_context(tc.tile_pool(name="stage", bufs=1))
         accs = ctx.enter_context(tc.psum_pool(name="accs", bufs=6))
         turns = ctx.enter_context(tc.psum_pool(name="turns", bufs=2))
 
         offsets = keep.tile([P, G * J // 16], U16, name="offsets")
         nc.sync.dma_start(offsets[:], offs)
 
-        tab_sc = keep.tile([P, T // 4], I32, name="tab_sc", align_bytes=64)
-        nc.vector.memset(tab_sc[:], 0)
-        iw_rows = keep.tile([P, P], F32, name="iw_rows")
-        nc.gpsimd.memset(iw_rows[:], 0.0)
         w_sc = keep.tile([P, PASSES, N // 4], I32, name="w_sc", align_bytes=64)
-        nc.vector.memset(w_sc[:], 0)
+        nc.gpsimd.memset(w_sc[:], 0)
+        tab_sc = keep.tile([P, T // 4], I32, name="tab_sc", align_bytes=64)
+        nc.vector.memset(tab_sc[:, : 5 * T // 32], 0)
+        nc.gpsimd.memset(tab_sc[:, 5 * T // 32 :], 0)
+        iw_rows = keep.tile([P, P], F32, name="iw_rows", align_bytes=64)
+        nc.gpsimd.memset(iw_rows[:], 0.0)
         wx_sc = keep.tile([P, PASSES, N // 4], I32, name="wx_sc", align_bytes=64)
         nc.vector.memset(wx_sc[:], 0)
-        moved = [keep.tile([P, 2 * J // 4], I32, name=f"moved{h}", align_bytes=64) for h in range(2)]
-        for h in range(2):
-            nc.vector.memset(moved[h][:], 0)
+        moved = keep.tile([P, G * J // 4], I32, name="moved", align_bytes=64)
+        nc.vector.memset(moved[96:P, :], 0)
 
-        def load_scales(engine, scales, plane):
-            for q in range(4):
+        def load_scales(engine, scales, plane, quadrants):
+            for q in quadrants:
                 engine.dma_start(
                     plane[32 * q : 32 * q + 4, :, :],
                     scales[:, 4 * q : 4 * q + 4, :].rearrange("a r n -> r a n").bitcast(I32),
@@ -59,39 +61,55 @@ def tile_list_interp_none_kernel(
         sc_rows = tab_scales.rearrange("a (q r) t -> r q a t", r=4)
         for r in range(4):
             nc.sync.dma_start(tab_sc[r:P:SHIFT, :], sc_rows[r].bitcast(I32))
-        w_c = keep.tile([P, PASSES, N], I32, name="w_c", align_bytes=64)
-        nc.sync.dma_start(w_c[:], w_words.rearrange("a p n i -> p a (n i)").bitcast(I32))
+        load_scales(nc.sync, w_scales, w_sc, range(1))
         tab_w = keep.tile([P, T], I32, name="tab_w", align_bytes=64)
         nc.sync.dma_start(tab_w[:], tab_words[0].rearrange("p t b -> p (t b)").bitcast(I32))
-        load_scales(nc.sync, w_scales, w_sc)
-        x_raw = [keep.tile([P, 4, J], F32, name=f"x_raw{a}") for a in range(PASSES)]
-        for a in range(PASSES):
-            nc.sync.dma_start(x_raw[a][:], x[512 * a : 512 * (a + 1), :].rearrange("(p i) j -> p i j", i=4))
+        w_c = keep.tile([P, PASSES, N], I32, name="w_c", align_bytes=64)
+        nc.sync.dma_start(w_c[:], w_words.rearrange("a p n i -> p a (n i)").bitcast(I32))
+        load_scales(nc.sync, w_scales, w_sc, range(1, 4))
+        H = J // 2
+        x_raw = {}
+
+        def load_x(h):
+            for a in range(PASSES):
+                x_raw[a, h] = stage.tile([P, 4, H], F32, name=f"x_raw{a}{h}", offset=4096 * (2 * h + a))
+                rows = x[512 * a : 512 * (a + 1), h * H : (h + 1) * H]
+                nc.sync.dma_start(x_raw[a, h][:], rows.rearrange("(p i) j -> p i j", i=4))
+
+        load_x(0)
+        for g, iw in enumerate((iw0, iw1, iw2, iw3)):
+            nc.gpsimd.dma_start(
+                iw_rows[g:P:32, :].rearrange("q (c m) -> q c m", m=32), iw.rearrange("(c q m) -> q c m", q=4, m=32)
+            )
         wx_c = keep.tile([P, PASSES, N], I32, name="wx_c", align_bytes=64)
         nc.sync.dma_start(wx_c[:], wx_words.rearrange("a p n i -> p a (n i)").bitcast(I32))
+        load_x(1)
+        load_scales(nc.sync, wx_scales, wx_sc, range(4))
 
-        for g, iw in enumerate((iw0, iw1, iw2, iw3)):
-            nc.gpsimd.dma_start(iw_rows[JT * g : JT * (g + 1), :], iw.rearrange("(c j) -> c j", j=P))
+
+        ones = keep.tile([P, P], F32, name="ones")
+        nc.vector.memset(ones[:], 1.0)
         ident = keep.tile([P, P], F32, name="ident")
-        make_identity(nc, ident[:])
-        load_scales(nc.gpsimd, wx_scales, wx_sc)
+        nc.vector.memset(ident[:], 0.0)
+        count = keep.tile([P, P], F32, name="count", align_bytes=64)
+        nc.vector.tensor_tensor_scan(count[:], ones[:], ones[:], 0.0, MULT, ADD)
+        count_t = keep.tile([P, P], F32, name="count_t", align_bytes=64)
+        nc.vector.transpose(count_t[:], count[:])
+        for q in range(4):
+            blk = slice(32 * q, 32 * (q + 1))
+            nc.vector.tensor_tensor(ident[blk, blk], count[blk, blk], count_t[blk, blk], EQ)
 
-        iw_ps = turns.tile([P, N], F32, name="turn", tag="turn")
-        nc.tensor.transpose(iw_ps[:, 0:P], iw_rows[:], ident[:])
-        iw_col = keep.tile([P, G * JT], F32, name="iw_col")
-        nc.scalar.copy(iw_col[:], iw_ps[:, 0 : G * JT])
 
         picked_sc = {}
         parted = {}
 
-        def gather_scales(h, tag):
-            gs = keep.tile([P, 2 * J], U8, name=f"picked_sc{h}", tag=tag, align_bytes=64)
-            nc.vector.tensor_copy(gs[:], tab_sc[:].bitcast(U8).indirect(offsets[:, 64 * h : 64 * (h + 1)]))
-            nc.scalar.dma_start(moved[h][0 : P - SHIFT, :], gs[SHIFT:P, :].bitcast(I32))
-            picked_sc[h] = gs
+        def gather_scales(g0, g1, gs, mover):
+            nc.vector.tensor_copy(gs[:], tab_sc[:].bitcast(U8).indirect(offsets[:, 32 * g0 : 32 * g1]))
+            mover.dma_start(moved[0 : P - SHIFT, g0 * J // 4 : g1 * J // 4], gs[SHIFT:P, :].bitcast(I32))
+            for g in range(g0, g1):
+                picked_sc[g] = gs[:, (g - g0) * J : (g - g0 + 1) * J]
 
-        def gather_words(g, tag):
-            gw = keep.tile([P, J], U32, name=f"picked_w{g}", tag=tag, align_bytes=64)
+        def gather_words(g, gw):
             nc.vector.tensor_copy(gw[:], tab_w[:].bitcast(U32).indirect(offsets[:, 32 * g : 32 * (g + 1)]))
             return gw
 
@@ -106,11 +124,10 @@ def tile_list_interp_none_kernel(
             parted[g] = pt
 
         def table_pass(acc, g, jt, a):
-            col = (g % 2) * J + jt * P
             if a == 0:
-                plane = picked_sc[g // 2][:, col : col + P]
+                plane = picked_sc[g][:, jt * P : (jt + 1) * P]
             else:
-                plane = moved[g // 2][:].bitcast(U8)[:, col : col + P]
+                plane = moved[:].bitcast(U8)[:, g * J + jt * P : g * J + (jt + 1) * P]
             nc.tensor.matmul_mx(
                 out=acc[:],
                 lhsT=parted[g][:, a, 2 * jt * P : 2 * (jt + 1) * P].bitcast(FP4X4),
@@ -122,12 +139,36 @@ def tile_list_interp_none_kernel(
             )
 
         def weight(g, jt):
-            return iw_col[:, JT * g + jt : JT * g + jt + 1]
+            return iw_col[:, 32 * jt + g : 32 * jt + g + 1]
 
-        gather_scales(0, "sc0")
-        gather_scales(1, "sc1")
-        part(0, gather_words(0, "w0"))
-        part(1, gather_words(1, "w1"))
+        gather_scales(0, 3, keep.tile([P, 3 * J], U8, name="picked_sc012", align_bytes=64), nc.scalar)
+        part(0, gather_words(0, reuse.tile([P, J], U32, name="picked_w0", align_bytes=64, offset=2048)))
+        iw_col = reuse.tile([P, P], F32, name="iw_col", align_bytes=64, offset=2560)
+        picked_w1 = gather_words(1, reuse.tile([P, J], U32, name="picked_w1", align_bytes=64, offset=512))
+        nc.vector.transpose(iw_col[:], iw_rows[:])
+        part(1, picked_w1)
+        gather_scales(3, 4, reuse.tile([P, J], U8, name="picked_sc3", align_bytes=64, offset=3072), nc.gpsimd)
+
+        x_c = keep.tile([P, PASSES, J], U32, name="x_c", align_bytes=64)
+        x_sc = keep.tile([P, PASSES, J], U8, name="x_sc", align_bytes=64)
+        x_bf = {}
+
+        def interleave_x(h):
+            for a in range(PASSES):
+                x_bf[a, h] = keep.tile([P, H, 4], BF16, name=f"xb{a}{h}", align_bytes=64)
+                nc.scalar.copy(
+                    x_bf[a, h][:].rearrange("p (c i) t -> p c t i", i=4),
+                    x_raw[a, h][:].rearrange("p t (c i) -> p c t i", i=4),
+                )
+
+        def quantize_x(a, h):
+            nc.vector.quantize_mx(
+                out=x_c[:, a, h * H : (h + 1) * H].bitcast(FP8X4),
+                scales=x_sc[:, a, h * H : (h + 1) * H],
+                in_=x_bf[a, h][:].rearrange("p c t -> p (c t)"),
+            )
+
+        interleave_x(0)
 
         scaled = {}
         acc0 = [accs.tile([P, N], F32, name="acc", tag="acc") for jt in range(JT)]
@@ -135,7 +176,7 @@ def tile_list_interp_none_kernel(
             for jt in range(JT):
                 table_pass(acc0[jt], 0, jt, a)
         for jt in range(JT):
-            s = keep.tile([P, N], F32, name=f"scaled0_{jt}")
+            s = stage.tile([P, N], F32, name=f"scaled0_{jt}", offset=2048 * jt)
             nc.scalar.activation(s[:], acc0[jt][:], COPY, scale=weight(0, jt))
             scaled[0, jt] = s
         for jt in range(JT):
@@ -146,27 +187,18 @@ def tile_list_interp_none_kernel(
             nc.scalar.activation(s[:], acc[:], COPY, scale=weight(1, jt))
             scaled[1, jt] = s
 
-        part(2, gather_words(2, "w2"))
-        part(3, gather_words(3, "w3"))
+        for g, offset in ((2, 3584), (3, 512)):
+            picked = gather_words(g, reuse.tile([P, J], U32, name=f"picked_w{g}", align_bytes=64, offset=offset))
+            quantize_x(g - 2, 0)
+            part(g, picked)
 
-        x_c = keep.tile([P, PASSES, J], U32, name="x_c", align_bytes=64)
-        x_sc = keep.tile([P, PASSES, J], U8, name="x_sc", align_bytes=64)
-        H = J // 2
-        for a in range(PASSES):
-            for h in range(2):
-                xb = keep.tile([P, H, 4], BF16, name=f"xb{a}{h}", align_bytes=64)
-                nc.scalar.copy(
-                    xb[:].rearrange("p (c i) t -> p c t i", i=4),
-                    x_raw[a][:, :, h * H : (h + 1) * H].rearrange("p t (c i) -> p c t i", i=4),
-                )
-                nc.vector.quantize_mx(
-                    out=x_c[:, a, h * H : (h + 1) * H].bitcast(FP8X4),
-                    scales=x_sc[:, a, h * H : (h + 1) * H],
-                    in_=xb[:].rearrange("p c t -> p (c t)"),
-                )
+        interleave_x(1)
 
         out_v = out.rearrange("(t p) j -> p t j", p=P)
         for jt in range(JT):
+            if jt == 1:
+                for a in range(PASSES):
+                    quantize_x(a, 1)
             total = scaled[1, jt]
             for g in (2, 3):
                 acc = accs.tile([P, N], F32, name="acc", tag="acc")

@@ -39,11 +39,11 @@ def tile_list_interp_none_kernel(
         offsets = keep.tile([P, G * J // 16], U16, name="offsets")
         nc.sync.dma_start(offsets[:], offs)
 
-        w_sc = keep.tile([P, PASSES, N // 4], I32, name="w_sc", align_bytes=64)
-        nc.gpsimd.memset(w_sc[:], 0)
         tab_sc = keep.tile([P, T // 4], I32, name="tab_sc", align_bytes=64)
-        nc.vector.memset(tab_sc[:, : 5 * T // 32], 0)
-        nc.gpsimd.memset(tab_sc[:, 5 * T // 32 :], 0)
+        nc.vector.memset(tab_sc[:, : T // 8], 0)
+        nc.gpsimd.memset(tab_sc[:, T // 8 :], 0)
+        w_sc = keep.tile([P, PASSES, N // 4], I32, name="w_sc", align_bytes=64)
+        nc.vector.memset(w_sc[:], 0)
         iw_rows = keep.tile([P, P], F32, name="iw_rows", align_bytes=64)
         nc.gpsimd.memset(iw_rows[:], 0.0)
         wx_sc = keep.tile([P, PASSES, N // 4], I32, name="wx_sc", align_bytes=64)
@@ -61,12 +61,13 @@ def tile_list_interp_none_kernel(
         sc_rows = tab_scales.rearrange("a (q r) t -> r q a t", r=4)
         for r in range(4):
             nc.sync.dma_start(tab_sc[r:P:SHIFT, :], sc_rows[r].bitcast(I32))
-        load_scales(nc.sync, w_scales, w_sc, range(1))
         tab_w = keep.tile([P, T], I32, name="tab_w", align_bytes=64)
-        nc.sync.dma_start(tab_w[:], tab_words[0].rearrange("p t b -> p (t b)").bitcast(I32))
+        tab_rows = tab_words[0].rearrange("p t b -> p (t b)").bitcast(I32)
+        for cols in (slice(0, T // 4), slice(T // 4, T)):
+            nc.sync.dma_start(tab_w[:, cols], tab_rows[:, cols])
         w_c = keep.tile([P, PASSES, N], I32, name="w_c", align_bytes=64)
         nc.sync.dma_start(w_c[:], w_words.rearrange("a p n i -> p a (n i)").bitcast(I32))
-        load_scales(nc.sync, w_scales, w_sc, range(1, 4))
+        load_scales(nc.sync, w_scales, w_sc, range(4))
         H = J // 2
         x_raw = {}
 
@@ -90,7 +91,7 @@ def tile_list_interp_none_kernel(
         ones = keep.tile([P, P], F32, name="ones")
         nc.vector.memset(ones[:], 1.0)
         ident = keep.tile([P, P], F32, name="ident")
-        nc.vector.memset(ident[:], 0.0)
+        nc.scalar.activation(ident[:], ones[:], COPY, scale=0.0)
         count = keep.tile([P, P], F32, name="count", align_bytes=64)
         nc.vector.tensor_tensor_scan(count[:], ones[:], ones[:], 0.0, MULT, ADD)
         count_t = keep.tile([P, P], F32, name="count_t", align_bytes=64)
@@ -157,8 +158,8 @@ def tile_list_interp_none_kernel(
             for a in range(PASSES):
                 x_bf[a, h] = keep.tile([P, H, 4], BF16, name=f"xb{a}{h}", align_bytes=64)
                 nc.scalar.copy(
-                    x_bf[a, h][:].rearrange("p (c i) t -> p c t i", i=4),
-                    x_raw[a, h][:].rearrange("p t (c i) -> p c t i", i=4),
+                    x_bf[a, h][:],
+                    x_raw[a, h][:].rearrange("p t c -> p c t"),
                 )
 
         def quantize_x(a, h):
@@ -195,18 +196,22 @@ def tile_list_interp_none_kernel(
         interleave_x(1)
 
         out_v = out.rearrange("(t p) j -> p t j", p=P)
+        sums = {}
+
+        def add_neighbour(g, jt):
+            acc = accs.tile([P, N], F32, name="acc", tag="acc")
+            for a in range(PASSES):
+                table_pass(acc, g, jt, a)
+            sums[g, jt] = keep.tile([P, N], F32, name=f"sum{g}_{jt}")
+            nc.vector.scalar_tensor_tensor(sums[g, jt][:], acc[:], weight(g, jt), scaled[g - 2, jt][:], MULT, ADD)
+
+        for jt in range(JT):
+            add_neighbour(2, jt)
         for jt in range(JT):
             if jt == 1:
                 for a in range(PASSES):
                     quantize_x(a, 1)
-            total = scaled[1, jt]
-            for g in (2, 3):
-                acc = accs.tile([P, N], F32, name="acc", tag="acc")
-                for a in range(PASSES):
-                    table_pass(acc, g, jt, a)
-                nxt = keep.tile([P, N], F32, name=f"sum{g}_{jt}")
-                nc.vector.scalar_tensor_tensor(nxt[:], acc[:], weight(g, jt), total[:], MULT, ADD)
-                total = nxt
+            add_neighbour(3, jt)
             acc = accs.tile([P, N], F32, name="acc", tag="acc")
             for a in range(PASSES):
                 nc.tensor.matmul_mx(
@@ -219,19 +224,27 @@ def tile_list_interp_none_kernel(
                     stop=(a == PASSES - 1),
                 )
             last = keep.tile([P, N], F32, name=f"sumx_{jt}")
-            nc.vector.tensor_tensor(last[:], acc[:], total[:], ADD)
-            turn = turns.tile([P, N], F32, name="turn", tag="turn")
-            terms = (scaled[0, jt], last)
-            for s, term in enumerate(terms):
-                for nt in range(NT):
-                    nc.tensor.matmul(
-                        turn[:, nt * P : (nt + 1) * P],
-                        term[:, nt * P : (nt + 1) * P],
-                        ident[:],
-                        start=(s == 0 and nt == 0),
-                        stop=(s == len(terms) - 1 and nt == NT - 1),
-                        is_transpose=True,
-                    )
             res = keep.tile([P, NT, P], F32, name=f"res{jt}")
-            nc.scalar.copy(res[:].rearrange("p t j -> p (t j)"), turn[:])
-            nc.sync.dma_start(out_v[:, :, jt * P : (jt + 1) * P], res[:])
+            pieces = 2 if jt == JT - 1 else 1
+            width = NT // pieces
+            for piece in range(pieces):
+                blocks = range(piece * width, (piece + 1) * width)
+                cols = slice(piece * width * P, (piece + 1) * width * P)
+                nc.vector.tensor_tensor(last[:, cols], acc[:, cols], sums[2, jt][:, cols], ADD)
+                turn = turns.tile([P, N], F32, name="turn", tag="turn")
+                for s, term in enumerate((sums[3, jt], last)):
+                    for i, nt in enumerate(blocks):
+                        nc.tensor.matmul(
+                            turn[:, i * P : (i + 1) * P],
+                            term[:, nt * P : (nt + 1) * P],
+                            ident[:],
+                            start=(s == 0 and i == 0),
+                            stop=(s == 1 and i == width - 1),
+                            is_transpose=True,
+                        )
+                part_res = res[:, blocks.start : blocks.stop, :]
+                if piece == 0:
+                    nc.scalar.copy(part_res.rearrange("p t j -> p (t j)"), turn[:, : width * P])
+                else:
+                    nc.vector.tensor_copy(part_res.rearrange("p t j -> p (t j)"), turn[:, : width * P])
+                nc.sync.dma_start(out_v[:, blocks.start : blocks.stop, jt * P : (jt + 1) * P], part_res)

@@ -23,6 +23,8 @@ ADD = mybir.AluOpType.add
 EQ = mybir.AluOpType.is_equal
 COPY = mybir.ActivationFunctionType.Copy
 SHIFT = 16
+X_RAW_AT = {(0, 0): 0, (1, 0): 4096, (0, 1): 12288, (1, 1): 16384}
+X_BF_AT = {(0, 0): (0, 2048), (1, 0): (2048, 2048), (0, 1): (4096, 2048), (1, 1): (6144, 10240)}
 
 
 def tile_list_interp_none_kernel(
@@ -33,8 +35,8 @@ def tile_list_interp_none_kernel(
         keep = ctx.enter_context(tc.tile_pool(name="keep", bufs=1))
         reuse = ctx.enter_context(tc.tile_pool(name="reuse", bufs=1))
         stage = ctx.enter_context(tc.tile_pool(name="stage", bufs=1))
-        accs = ctx.enter_context(tc.psum_pool(name="accs", bufs=6))
-        turns = ctx.enter_context(tc.psum_pool(name="turns", bufs=2))
+        late = ctx.enter_context(tc.tile_pool(name="late", bufs=1))
+        banks = ctx.enter_context(tc.psum_pool(name="banks", bufs=1))
 
         offsets = keep.tile([P, G * J // 16], U16, name="offsets")
         nc.sync.dma_start(offsets[:], offs)
@@ -71,22 +73,21 @@ def tile_list_interp_none_kernel(
         H = J // 2
         x_raw = {}
 
-        def load_x(h):
-            for a in range(PASSES):
-                x_raw[a, h] = stage.tile([P, 4, H], F32, name=f"x_raw{a}{h}", offset=4096 * (2 * h + a))
-                rows = x[512 * a : 512 * (a + 1), h * H : (h + 1) * H]
-                nc.sync.dma_start(x_raw[a, h][:], rows.rearrange("(p i) j -> p i j", i=4))
+        def load_x(a, h, planes=4):
+            held = stage.tile([P, planes, H], F32, name=f"x_raw{a}{h}", offset=X_RAW_AT[a, h])
+            x_raw[a, h] = held[:, 0:4, :]
+            rows = x[512 * a : 512 * (a + 1), h * H : (h + 1) * H]
+            nc.sync.dma_start(x_raw[a, h], rows.rearrange("(p i) j -> p i j", i=4))
 
-        load_x(0)
+        load_x(0, 0)
+        load_x(1, 0, planes=8)
         for g, iw in enumerate((iw0, iw1, iw2, iw3)):
             nc.gpsimd.dma_start(
                 iw_rows[g:P:32, :].rearrange("q (c m) -> q c m", m=32), iw.rearrange("(c q m) -> q c m", q=4, m=32)
             )
         wx_c = keep.tile([P, PASSES, N], I32, name="wx_c", align_bytes=64)
         nc.sync.dma_start(wx_c[:], wx_words.rearrange("a p n i -> p a (n i)").bitcast(I32))
-        load_x(1)
-        load_scales(nc.sync, wx_scales, wx_sc, range(4))
-
+        load_scales(nc.gpsimd, wx_scales, wx_sc, range(4))
 
         ones = keep.tile([P, P], F32, name="ones")
         nc.vector.memset(ones[:], 1.0)
@@ -99,7 +100,6 @@ def tile_list_interp_none_kernel(
         for q in range(4):
             blk = slice(32 * q, 32 * (q + 1))
             nc.vector.tensor_tensor(ident[blk, blk], count[blk, blk], count_t[blk, blk], EQ)
-
 
         picked_sc = {}
         parted = {}
@@ -139,16 +139,29 @@ def tile_list_interp_none_kernel(
                 stop=(a == PASSES - 1),
             )
 
+        def bank(number):
+            return banks.tile([P, N], F32, name=f"bank{number}", tag=f"bank{number}")
+
+        def table_products(g, tiles, first_bank):
+            accs = {jt: bank(first_bank + i) for i, jt in enumerate(tiles)}
+            for a in range(PASSES):
+                for jt in tiles:
+                    table_pass(accs[jt], g, jt, a)
+            return accs
+
         def weight(g, jt):
             return iw_col[:, 32 * jt + g : 32 * jt + g + 1]
 
-        gather_scales(0, 3, keep.tile([P, 3 * J], U8, name="picked_sc012", align_bytes=64), nc.scalar)
+        gather_scales(0, 2, keep.tile([P, 2 * J], U8, name="picked_sc01", align_bytes=64), nc.scalar)
         part(0, gather_words(0, reuse.tile([P, J], U32, name="picked_w0", align_bytes=64, offset=2048)))
         iw_col = reuse.tile([P, P], F32, name="iw_col", align_bytes=64, offset=2560)
         picked_w1 = gather_words(1, reuse.tile([P, J], U32, name="picked_w1", align_bytes=64, offset=512))
         nc.vector.transpose(iw_col[:], iw_rows[:])
         part(1, picked_w1)
-        gather_scales(3, 4, reuse.tile([P, J], U8, name="picked_sc3", align_bytes=64, offset=3072), nc.gpsimd)
+        gather_scales(2, 3, reuse.tile([P, J], U8, name="picked_sc2", align_bytes=64, offset=3072), nc.sync)
+        load_x(0, 1)
+        load_x(1, 1)
+        part(2, gather_words(2, reuse.tile([P, J], U32, name="picked_w2", align_bytes=64, offset=3584)))
 
         x_c = keep.tile([P, PASSES, J], U32, name="x_c", align_bytes=64)
         x_sc = keep.tile([P, PASSES, J], U8, name="x_sc", align_bytes=64)
@@ -156,63 +169,21 @@ def tile_list_interp_none_kernel(
 
         def interleave_x(h):
             for a in range(PASSES):
-                x_bf[a, h] = keep.tile([P, H, 4], BF16, name=f"xb{a}{h}", align_bytes=64)
-                nc.scalar.copy(
-                    x_bf[a, h][:],
-                    x_raw[a, h][:].rearrange("p t c -> p c t"),
+                at, span = X_BF_AT[a, h]
+                held = late.tile([P, span // 8, 4], BF16, name=f"xb{a}{h}", align_bytes=64, offset=at)
+                x_bf[a, h] = held[:, 0:H, :]
+                nc.scalar.copy(x_bf[a, h], x_raw[a, h].rearrange("p t c -> p c t"))
+
+        def quantize_x(h):
+            for a in range(PASSES):
+                nc.vector.quantize_mx(
+                    out=x_c[:, a, h * H : (h + 1) * H].bitcast(FP8X4),
+                    scales=x_sc[:, a, h * H : (h + 1) * H],
+                    in_=x_bf[a, h].rearrange("p c t -> p (c t)"),
                 )
 
-        def quantize_x(a, h):
-            nc.vector.quantize_mx(
-                out=x_c[:, a, h * H : (h + 1) * H].bitcast(FP8X4),
-                scales=x_sc[:, a, h * H : (h + 1) * H],
-                in_=x_bf[a, h][:].rearrange("p c t -> p (c t)"),
-            )
-
-        interleave_x(0)
-
-        scaled = {}
-        acc0 = [accs.tile([P, N], F32, name="acc", tag="acc") for jt in range(JT)]
-        for a in range(PASSES):
-            for jt in range(JT):
-                table_pass(acc0[jt], 0, jt, a)
-        for jt in range(JT):
-            s = stage.tile([P, N], F32, name=f"scaled0_{jt}", offset=2048 * jt)
-            nc.scalar.activation(s[:], acc0[jt][:], COPY, scale=weight(0, jt))
-            scaled[0, jt] = s
-        for jt in range(JT):
-            acc = accs.tile([P, N], F32, name="acc", tag="acc")
-            for a in range(PASSES):
-                table_pass(acc, 1, jt, a)
-            s = keep.tile([P, N], F32, name=f"scaled1_{jt}")
-            nc.scalar.activation(s[:], acc[:], COPY, scale=weight(1, jt))
-            scaled[1, jt] = s
-
-        for g, offset in ((2, 3584), (3, 512)):
-            picked = gather_words(g, reuse.tile([P, J], U32, name=f"picked_w{g}", align_bytes=64, offset=offset))
-            quantize_x(g - 2, 0)
-            part(g, picked)
-
-        interleave_x(1)
-
-        out_v = out.rearrange("(t p) j -> p t j", p=P)
-        sums = {}
-
-        def add_neighbour(g, jt):
-            acc = accs.tile([P, N], F32, name="acc", tag="acc")
-            for a in range(PASSES):
-                table_pass(acc, g, jt, a)
-            sums[g, jt] = keep.tile([P, N], F32, name=f"sum{g}_{jt}")
-            nc.vector.scalar_tensor_tensor(sums[g, jt][:], acc[:], weight(g, jt), scaled[g - 2, jt][:], MULT, ADD)
-
-        for jt in range(JT):
-            add_neighbour(2, jt)
-        for jt in range(JT):
-            if jt == 1:
-                for a in range(PASSES):
-                    quantize_x(a, 1)
-            add_neighbour(3, jt)
-            acc = accs.tile([P, N], F32, name="acc", tag="acc")
+        def x_product(jt, number):
+            acc = bank(number)
             for a in range(PASSES):
                 nc.tensor.matmul_mx(
                     out=acc[:],
@@ -223,28 +194,75 @@ def tile_list_interp_none_kernel(
                     start=(a == 0),
                     stop=(a == PASSES - 1),
                 )
-            last = keep.tile([P, N], F32, name=f"sumx_{jt}")
-            res = keep.tile([P, NT, P], F32, name=f"res{jt}")
-            pieces = 2 if jt == JT - 1 else 1
-            width = NT // pieces
-            for piece in range(pieces):
-                blocks = range(piece * width, (piece + 1) * width)
-                cols = slice(piece * width * P, (piece + 1) * width * P)
-                nc.vector.tensor_tensor(last[:, cols], acc[:, cols], sums[2, jt][:, cols], ADD)
-                turn = turns.tile([P, N], F32, name="turn", tag="turn")
-                for s, term in enumerate((sums[3, jt], last)):
-                    for i, nt in enumerate(blocks):
-                        nc.tensor.matmul(
-                            turn[:, i * P : (i + 1) * P],
-                            term[:, nt * P : (nt + 1) * P],
-                            ident[:],
-                            start=(s == 0 and i == 0),
-                            stop=(s == 1 and i == width - 1),
-                            is_transpose=True,
-                        )
-                part_res = res[:, blocks.start : blocks.stop, :]
-                if piece == 0:
-                    nc.scalar.copy(part_res.rearrange("p t j -> p (t j)"), turn[:, : width * P])
-                else:
-                    nc.vector.tensor_copy(part_res.rearrange("p t j -> p (t j)"), turn[:, : width * P])
-                nc.sync.dma_start(out_v[:, blocks.start : blocks.stop, jt * P : (jt + 1) * P], part_res)
+            return acc
+
+        interleave_x(0)
+        quantize_x(0)
+        gather_scales(3, 4, late.tile([P, J], U8, name="picked_sc3", align_bytes=64, offset=X_BF_AT[0, 0][0]), nc.sync)
+        part(3, gather_words(3, late.tile([P, J], U32, name="picked_w3", align_bytes=64, offset=X_BF_AT[1, 0][0])))
+
+        scaled = {}
+        acc0 = table_products(0, range(JT), 0)
+        for jt in range(JT):
+            scaled[0, jt] = stage.tile([P, N], F32, name=f"scaled0_{jt}", offset=X_RAW_AT[1, 0] + 2048 * jt)
+            nc.scalar.activation(scaled[0, jt][:], acc0[jt][:], COPY, scale=weight(0, jt))
+        for jt in range(JT):
+            acc = table_products(1, [jt], JT + jt)[jt]
+            scaled[1, jt] = keep.tile([P, N], F32, name=f"scaled1_{jt}")
+            nc.scalar.activation(scaled[1, jt][:], acc[:], COPY, scale=weight(1, jt))
+        interleave_x(1)
+
+        out_v = out.rearrange("(t p) j -> p t j", p=P)
+
+        def weigh_and_add(g, jt, acc, term, dst):
+            nc.vector.scalar_tensor_tensor(dst[:], acc[:], weight(g, jt), term[:], MULT, ADD)
+            return dst
+
+        def turn_and_store(jt, terms, blocks, copier, number):
+            width = len(blocks)
+            turn = bank(number)
+            for s, term in enumerate(terms):
+                for i, nt in enumerate(blocks):
+                    nc.tensor.matmul(
+                        turn[:, i * P : (i + 1) * P],
+                        term[:, nt * P : (nt + 1) * P],
+                        ident[:],
+                        start=(s == 0 and i == 0),
+                        stop=(s == len(terms) - 1 and i == width - 1),
+                        is_transpose=True,
+                    )
+            res = keep.tile([P, width, P], F32, name=f"res{jt}_{blocks.start}")
+            copier(res[:].rearrange("p t j -> p (t j)"), turn[:, : width * P])
+            nc.sync.dma_start(out_v[:, blocks.start : blocks.stop, jt * P : (jt + 1) * P], res[:])
+
+        def held_tile(name, slot):
+            return late.tile([P, N], F32, name=name, offset=X_BF_AT[0, 1][0] + 2048 * slot)
+
+        acc2 = table_products(2, range(JT), 0)
+        with_x, with2, with3 = {}, {}, {}
+        for jt in (0, 1):
+            with_x[jt] = keep.tile([P, N], F32, name=f"with_x{jt}")
+            nc.vector.tensor_tensor(with_x[jt][:], x_product(jt, JT + jt)[:], scaled[0, jt][:], ADD)
+        acc3 = table_products(3, (0, 1), 6)
+        for jt in (0, 1):
+            with2[jt] = weigh_and_add(2, jt, acc2[jt], scaled[1, jt], keep.tile([P, N], F32, name=f"with2_{jt}"))
+        for jt in (2, 3):
+            acc3[jt] = table_products(3, [jt], 2 + jt)[jt]
+        quantize_x(1)
+        accx = {jt: x_product(jt, jt - 2) for jt in (2, 3)}
+        for jt in (0, 1):
+            with3[jt] = weigh_and_add(3, jt, acc3[jt], with_x[jt], held_tile(f"with3_{jt}", jt))
+            turn_and_store(jt, (with2[jt], with3[jt]), range(NT), nc.scalar.copy, 6 + jt)
+        for jt in (2, 3):
+            with2[jt] = keep.tile([P, N], F32, name=f"with2_{jt}")
+            nc.scalar.activation(with2[jt][:], acc2[jt][:], COPY, scale=weight(2, jt))
+        for jt in (2, 3):
+            with3[jt] = weigh_and_add(3, jt, acc3[jt], scaled[0, jt], held_tile(f"with3_{jt}", jt))
+        with_x[2] = keep.tile([P, N], F32, name="with_x2")
+        nc.vector.tensor_tensor(with_x[2][:], accx[2][:], scaled[1, 2][:], ADD)
+        turn_and_store(2, (with2[2], with3[2], with_x[2]), range(NT), nc.scalar.copy, 2)
+        with_x[3] = keep.tile([P, N], F32, name="with_x3")
+        for blocks, copier, number in ((range(0, 2), nc.scalar.copy, 3), (range(2, 4), nc.vector.tensor_copy, 4)):
+            cols = slice(blocks.start * P, blocks.stop * P)
+            nc.vector.tensor_tensor(with_x[3][:, cols], accx[3][:, cols], scaled[1, 3][:, cols], ADD)
+            turn_and_store(3, (with2[3], with3[3], with_x[3]), blocks, copier, number)

@@ -23,7 +23,7 @@ ADD = mybir.AluOpType.add
 EQ = mybir.AluOpType.is_equal
 COPY = mybir.ActivationFunctionType.Copy
 SHIFT = 16
-X_RAW_AT = {(0, 0): 0, (1, 0): 4096, (0, 1): 12288, (1, 1): 16384}
+X_RAW_AT = {(0, 0): 0, (1, 0): 4096, (0, 1): 20480, (1, 1): 24576}
 X_BF_AT = {(0, 0): (0, 2048), (1, 0): (2048, 2048), (0, 1): (4096, 2048), (1, 1): (6144, 10240)}
 
 
@@ -80,7 +80,7 @@ def tile_list_interp_none_kernel(
             nc.sync.dma_start(x_raw[a, h], rows.rearrange("(p i) j -> p i j", i=4))
 
         load_x(0, 0)
-        load_x(1, 0, planes=8)
+        load_x(1, 0, planes=16)
         for g, iw in enumerate((iw0, iw1, iw2, iw3)):
             nc.gpsimd.dma_start(
                 iw_rows[g:P:32, :].rearrange("q (c m) -> q c m", m=32), iw.rearrange("(c q m) -> q c m", q=4, m=32)
@@ -115,7 +115,10 @@ def tile_list_interp_none_kernel(
             return gw
 
         def part(g, gw):
-            pt = keep.tile([P, PASSES, 2 * J], U8, name=f"parted{g}", align_bytes=64)
+            if g in (1, 2):
+                pt = late.tile([P, PASSES, 2 * J], U8, name=f"parted{g}", align_bytes=64, offset=X_BF_AT[g - 1, 1][0])
+            else:
+                pt = keep.tile([P, PASSES, 2 * J], U8, name=f"parted{g}", align_bytes=64)
             src = gw[:].bitcast(U16).rearrange("p (j d) -> p d j", d=PASSES)
             if g == 0:
                 for a in range(PASSES):
@@ -152,16 +155,17 @@ def tile_list_interp_none_kernel(
         def weight(g, jt):
             return iw_col[:, 32 * jt + g : 32 * jt + g + 1]
 
-        gather_scales(0, 2, keep.tile([P, 2 * J], U8, name="picked_sc01", align_bytes=64), nc.scalar)
+        gather_scales(0, 3, keep.tile([P, 3 * J], U8, name="picked_sc012", align_bytes=64), nc.scalar)
         part(0, gather_words(0, reuse.tile([P, J], U32, name="picked_w0", align_bytes=64, offset=2048)))
         iw_col = reuse.tile([P, P], F32, name="iw_col", align_bytes=64, offset=2560)
         picked_w1 = gather_words(1, reuse.tile([P, J], U32, name="picked_w1", align_bytes=64, offset=512))
         nc.vector.transpose(iw_col[:], iw_rows[:])
         part(1, picked_w1)
-        gather_scales(2, 3, reuse.tile([P, J], U8, name="picked_sc2", align_bytes=64, offset=3072), nc.sync)
+        picked_w2 = gather_words(2, reuse.tile([P, J], U32, name="picked_w2", align_bytes=64, offset=3584))
         load_x(0, 1)
+        gather_scales(3, 4, reuse.tile([P, J], U8, name="picked_sc3", align_bytes=64, offset=3072), nc.sync)
         load_x(1, 1)
-        part(2, gather_words(2, reuse.tile([P, J], U32, name="picked_w2", align_bytes=64, offset=3584)))
+        part(2, picked_w2)
 
         x_c = keep.tile([P, PASSES, J], U32, name="x_c", align_bytes=64)
         x_sc = keep.tile([P, PASSES, J], U8, name="x_sc", align_bytes=64)
@@ -197,9 +201,8 @@ def tile_list_interp_none_kernel(
             return acc
 
         interleave_x(0)
+        part(3, gather_words(3, reuse.tile([P, J], U32, name="picked_w3", align_bytes=64, offset=4096)))
         quantize_x(0)
-        gather_scales(3, 4, late.tile([P, J], U8, name="picked_sc3", align_bytes=64, offset=X_BF_AT[0, 0][0]), nc.sync)
-        part(3, gather_words(3, late.tile([P, J], U32, name="picked_w3", align_bytes=64, offset=X_BF_AT[1, 0][0])))
 
         scaled = {}
         acc0 = table_products(0, range(JT), 0)
@@ -208,7 +211,7 @@ def tile_list_interp_none_kernel(
             nc.scalar.activation(scaled[0, jt][:], acc0[jt][:], COPY, scale=weight(0, jt))
         for jt in range(JT):
             acc = table_products(1, [jt], JT + jt)[jt]
-            scaled[1, jt] = keep.tile([P, N], F32, name=f"scaled1_{jt}")
+            scaled[1, jt] = stage.tile([P, N], F32, name=f"scaled1_{jt}", offset=X_RAW_AT[1, 0] + 2048 * (JT + jt))
             nc.scalar.activation(scaled[1, jt][:], acc[:], COPY, scale=weight(1, jt))
         interleave_x(1)
 
@@ -239,30 +242,35 @@ def tile_list_interp_none_kernel(
             return late.tile([P, N], F32, name=name, offset=X_BF_AT[0, 1][0] + 2048 * slot)
 
         acc2 = table_products(2, range(JT), 0)
-        with_x, with2, with3 = {}, {}, {}
+        with_x, with2, with3, acc3, accx = {}, {}, {}, {}, {}
+
+        def add_x(jt, acc, term, dst, cols=slice(0, N)):
+            nc.vector.tensor_tensor(dst[:, cols], acc[:, cols], term[:, cols], ADD)
+            return dst
+
         for jt in (0, 1):
-            with_x[jt] = keep.tile([P, N], F32, name=f"with_x{jt}")
-            nc.vector.tensor_tensor(with_x[jt][:], x_product(jt, JT + jt)[:], scaled[0, jt][:], ADD)
-        acc3 = table_products(3, (0, 1), 6)
+            acc3[jt] = table_products(3, [jt], JT + jt)[jt]
+            with2[jt] = weigh_and_add(2, jt, acc2[jt], scaled[0, jt], keep.tile([P, N], F32, name=f"with2_{jt}"))
         for jt in (0, 1):
-            with2[jt] = weigh_and_add(2, jt, acc2[jt], scaled[1, jt], keep.tile([P, N], F32, name=f"with2_{jt}"))
-        for jt in (2, 3):
-            acc3[jt] = table_products(3, [jt], 2 + jt)[jt]
+            accx[jt] = x_product(jt, jt)
+            if jt == 0:
+                acc3[2] = table_products(3, [2], JT + 2)[2]
+        for jt in (0, 1):
+            with3[jt] = weigh_and_add(3, jt, acc3[jt], scaled[1, jt], keep.tile([P, N], F32, name=f"with3_{jt}"))
+            with_x[jt] = add_x(jt, accx[jt], with2[jt], keep.tile([P, N], F32, name=f"with_x{jt}"))
+            turn_and_store(jt, (with3[jt], with_x[jt]), range(NT), nc.scalar.copy, JT + jt)
+            if jt == 0:
+                acc3[3] = table_products(3, [3], JT + 3)[3]
         quantize_x(1)
-        accx = {jt: x_product(jt, jt - 2) for jt in (2, 3)}
-        for jt in (0, 1):
-            with3[jt] = weigh_and_add(3, jt, acc3[jt], with_x[jt], held_tile(f"with3_{jt}", jt))
-            turn_and_store(jt, (with2[jt], with3[jt]), range(NT), nc.scalar.copy, 6 + jt)
         for jt in (2, 3):
             with2[jt] = keep.tile([P, N], F32, name=f"with2_{jt}")
             nc.scalar.activation(with2[jt][:], acc2[jt][:], COPY, scale=weight(2, jt))
+            accx[jt] = x_product(jt, jt)
         for jt in (2, 3):
-            with3[jt] = weigh_and_add(3, jt, acc3[jt], scaled[0, jt], held_tile(f"with3_{jt}", jt))
-        with_x[2] = keep.tile([P, N], F32, name="with_x2")
-        nc.vector.tensor_tensor(with_x[2][:], accx[2][:], scaled[1, 2][:], ADD)
-        turn_and_store(2, (with2[2], with3[2], with_x[2]), range(NT), nc.scalar.copy, 2)
+            with3[jt] = weigh_and_add(3, jt, acc3[jt], scaled[0, jt], held_tile(f"with3_{jt}", jt - 1))
+        with_x[2] = add_x(2, accx[2], scaled[1, 2], keep.tile([P, N], F32, name="with_x2"))
+        turn_and_store(2, (with2[2], with3[2], with_x[2]), range(NT), nc.scalar.copy, 0)
         with_x[3] = keep.tile([P, N], F32, name="with_x3")
-        for blocks, copier, number in ((range(0, 2), nc.scalar.copy, 3), (range(2, 4), nc.vector.tensor_copy, 4)):
-            cols = slice(blocks.start * P, blocks.stop * P)
-            nc.vector.tensor_tensor(with_x[3][:, cols], accx[3][:, cols], scaled[1, 3][:, cols], ADD)
+        for blocks, copier, number in ((range(0, 2), nc.scalar.copy, 1), (range(2, 4), nc.vector.tensor_copy, 6)):
+            add_x(3, accx[3], scaled[1, 3], with_x[3], slice(blocks.start * P, blocks.stop * P))
             turn_and_store(3, (with2[3], with3[3], with_x[3]), blocks, copier, number)

@@ -39,7 +39,6 @@ def tile_list_interp_none_kernel(
         banks = ctx.enter_context(tc.psum_pool(name="banks", bufs=1))
 
         offsets = keep.tile([P, G * J // 16], U16, name="offsets")
-        nc.sync.dma_start(offsets[:], offs)
 
         tab_sc = keep.tile([P, T // 4], I32, name="tab_sc", align_bytes=64)
         nc.vector.memset(tab_sc[:, : T // 8], 0)
@@ -60,13 +59,14 @@ def tile_list_interp_none_kernel(
                     scales[:, 4 * q : 4 * q + 4, :].rearrange("a r n -> r a n").bitcast(I32),
                 )
 
+        tab_w = keep.tile([P, T], I32, name="tab_w", align_bytes=64)
+        tab_rows = tab_words[0].rearrange("p t b -> p (t b)").bitcast(I32)
+        nc.sync.dma_start(tab_w[:, : T // 8], tab_rows[:, : T // 8])
+        nc.sync.dma_start(offsets[:], offs)
         sc_rows = tab_scales.rearrange("a (q r) t -> r q a t", r=4)
         for r in range(4):
             nc.sync.dma_start(tab_sc[r:P:SHIFT, :], sc_rows[r].bitcast(I32))
-        tab_w = keep.tile([P, T], I32, name="tab_w", align_bytes=64)
-        tab_rows = tab_words[0].rearrange("p t b -> p (t b)").bitcast(I32)
-        for cols in (slice(0, T // 4), slice(T // 4, T)):
-            nc.sync.dma_start(tab_w[:, cols], tab_rows[:, cols])
+        nc.sync.dma_start(tab_w[:, T // 8 :], tab_rows[:, T // 8 :])
         w_c = keep.tile([P, PASSES, N], I32, name="w_c", align_bytes=64)
         nc.sync.dma_start(w_c[:], w_words.rearrange("a p n i -> p a (n i)").bitcast(I32))
         load_scales(nc.sync, w_scales, w_sc, range(4))
@@ -121,8 +121,8 @@ def tile_list_interp_none_kernel(
                 pt = keep.tile([P, PASSES, 2 * J], U8, name=f"parted{g}", align_bytes=64)
             src = gw[:].bitcast(U16).rearrange("p (j d) -> p d j", d=PASSES)
             if g == 0:
-                for a in range(PASSES):
-                    nc.vector.tensor_copy(pt[:, a, :].bitcast(U16), src[:, a, :])
+                for a, cols in ((0, slice(0, P)), (0, slice(P, J)), (1, slice(0, J))):
+                    nc.vector.tensor_copy(pt[:, a, :].bitcast(U16)[:, cols], src[:, a, cols])
             else:
                 nc.vector.tensor_copy(pt[:].bitcast(U16), src)
             parted[g] = pt
@@ -176,7 +176,10 @@ def tile_list_interp_none_kernel(
                 at, span = X_BF_AT[a, h]
                 held = late.tile([P, span // 8, 4], BF16, name=f"xb{a}{h}", align_bytes=64, offset=at)
                 x_bf[a, h] = held[:, 0:H, :]
-                nc.scalar.copy(x_bf[a, h], x_raw[a, h].rearrange("p t c -> p c t"))
+                nc.scalar.copy(
+                    x_bf[a, h].rearrange("p (c i) t -> p c t i", i=4),
+                    x_raw[a, h].rearrange("p t (c i) -> p c t i", i=4),
+                )
 
         def quantize_x(h):
             for a in range(PASSES):
@@ -263,14 +266,18 @@ def tile_list_interp_none_kernel(
                 acc3[3] = table_products(3, [3], JT + 3)[3]
         quantize_x(1)
         for jt in (2, 3):
-            with2[jt] = keep.tile([P, N], F32, name=f"with2_{jt}")
-            nc.scalar.activation(with2[jt][:], acc2[jt][:], COPY, scale=weight(2, jt))
+            if jt == 2:
+                with2[jt] = weigh_and_add(2, jt, acc2[jt], scaled[1, jt], held_tile("with2_2", 0))
+            else:
+                with2[jt] = keep.tile([P, N], F32, name=f"with2_{jt}")
+                nc.scalar.activation(with2[jt][:], acc2[jt][:], COPY, scale=weight(2, jt))
             accx[jt] = x_product(jt, jt)
         for jt in (2, 3):
             with3[jt] = weigh_and_add(3, jt, acc3[jt], scaled[0, jt], held_tile(f"with3_{jt}", jt - 1))
-        with_x[2] = add_x(2, accx[2], scaled[1, 2], keep.tile([P, N], F32, name="with_x2"))
-        turn_and_store(2, (with2[2], with3[2], with_x[2]), range(NT), nc.scalar.copy, 0)
+        with_x[2] = add_x(2, accx[2], with2[2], keep.tile([P, N], F32, name="with_x2"))
+        turn_and_store(2, (with3[2], with_x[2]), range(NT), nc.scalar.copy, 0)
         with_x[3] = keep.tile([P, N], F32, name="with_x3")
-        for blocks, copier, number in ((range(0, 2), nc.scalar.copy, 1), (range(2, 4), nc.vector.tensor_copy, 6)):
-            add_x(3, accx[3], scaled[1, 3], with_x[3], slice(blocks.start * P, blocks.stop * P))
+        for half in range(2):
+            add_x(3, accx[3], scaled[1, 3], with_x[3], slice(half * N // 2, (half + 1) * N // 2))
+        for blocks, copier, number in ((range(0, 2), nc.scalar.copy, 1), (range(2, 4), nc.vector.tensor_copy, 3)):
             turn_and_store(3, (with2[3], with3[3], with_x[3]), blocks, copier, number)

@@ -20,9 +20,10 @@ FP8X4 = mybir.dt.float8_e4m3fn_x4
 FP4X4 = mybir.dt.float4_e2m1fn_x4
 MULT = mybir.AluOpType.mult
 ADD = mybir.AluOpType.add
-EQ = mybir.AluOpType.is_equal
+ABS = mybir.ActivationFunctionType.Abs
+RELU = mybir.ActivationFunctionType.Relu
 COPY = mybir.ActivationFunctionType.Copy
-SHIFT = 16
+SC_AT = 96
 X_RAW_AT = {(0, 0): 0, (1, 0): 4096, (0, 1): 20480, (1, 1): 24576}
 X_BF_AT = {(0, 0): (0, 2048), (1, 0): (2048, 2048), (0, 1): (4096, 2048), (1, 1): (6144, 10240)}
 
@@ -36,21 +37,28 @@ def tile_list_interp_none_kernel(
         reuse = ctx.enter_context(tc.tile_pool(name="reuse", bufs=1))
         stage = ctx.enter_context(tc.tile_pool(name="stage", bufs=1))
         late = ctx.enter_context(tc.tile_pool(name="late", bufs=1))
+        rows = ctx.enter_context(tc.tile_pool(name="rows", bufs=1))
         banks = ctx.enter_context(tc.psum_pool(name="banks", bufs=1))
 
         offsets = keep.tile([P, G * J // 16], U16, name="offsets")
 
-        tab_sc = keep.tile([P, T // 4], I32, name="tab_sc", align_bytes=64)
-        nc.vector.memset(tab_sc[:, : T // 8], 0)
-        nc.gpsimd.memset(tab_sc[:, T // 8 :], 0)
         w_sc = keep.tile([P, PASSES, N // 4], I32, name="w_sc", align_bytes=64)
-        nc.vector.memset(w_sc[:], 0)
-        iw_rows = keep.tile([P, P], F32, name="iw_rows", align_bytes=64)
-        nc.gpsimd.memset(iw_rows[:], 0.0)
+        nc.gpsimd.memset(w_sc[:], 0)
+        tab_sc = rows.tile([P, T // 4], I32, name="tab_sc", align_bytes=64, offset=0)
+        nc.vector.memset(tab_sc[0:SC_AT, :], 0)
+        planes01 = keep.tile([P, PASSES, 2 * J // 4], I32, name="planes01", align_bytes=64)
+        nc.vector.memset(planes01[:], 0)
         wx_sc = keep.tile([P, PASSES, N // 4], I32, name="wx_sc", align_bytes=64)
-        nc.vector.memset(wx_sc[:], 0)
-        moved = keep.tile([P, G * J // 4], I32, name="moved", align_bytes=64)
-        nc.vector.memset(moved[96:P, :], 0)
+        planes23 = rows.tile([P, PASSES, 2 * J // 4], I32, name="planes23", align_bytes=64, offset=0)
+        iw_rows = late.tile([P, P], F32, name="iw_rows", align_bytes=64, offset=X_BF_AT[1, 1][0])
+        nc.gpsimd.memset(iw_rows[:], 0.0)
+        nc.gpsimd.memset(wx_sc[:], 0)
+        apart = keep.tile([P, P], F32, name="apart")
+        nc.gpsimd.iota(apart[:], [[1, P]], base=0, channel_multiplier=-1, allow_small_or_imprecise_dtypes=True)
+        distance = keep.tile([P, P], F32, name="distance")
+        nc.scalar.activation(distance[:], apart[:], ABS)
+        ident = keep.tile([P, P], F32, name="ident")
+        nc.scalar.activation(ident[:], distance[:], RELU, bias=1.0, scale=-1.0)
 
         def load_scales(engine, scales, plane, quadrants):
             for q in quadrants:
@@ -61,54 +69,39 @@ def tile_list_interp_none_kernel(
 
         tab_w = keep.tile([P, T], I32, name="tab_w", align_bytes=64)
         tab_rows = tab_words[0].rearrange("p t b -> p (t b)").bitcast(I32)
-        nc.sync.dma_start(tab_w[:, : T // 8], tab_rows[:, : T // 8])
+        nc.sync.dma_start(tab_sc[SC_AT:P, :], tab_scales.rearrange("a q t -> (a q) t").bitcast(I32))
         nc.sync.dma_start(offsets[:], offs)
-        sc_rows = tab_scales.rearrange("a (q r) t -> r q a t", r=4)
-        for r in range(4):
-            nc.sync.dma_start(tab_sc[r:P:SHIFT, :], sc_rows[r].bitcast(I32))
-        nc.sync.dma_start(tab_w[:, T // 8 :], tab_rows[:, T // 8 :])
+        nc.sync.dma_start(tab_w[:], tab_rows)
         w_c = keep.tile([P, PASSES, N], I32, name="w_c", align_bytes=64)
-        nc.sync.dma_start(w_c[:], w_words.rearrange("a p n i -> p a (n i)").bitcast(I32))
-        load_scales(nc.sync, w_scales, w_sc, range(4))
+        wx_c = keep.tile([P, PASSES, N], I32, name="wx_c", align_bytes=64)
         H = J // 2
         x_raw = {}
 
         def load_x(a, h, planes=4):
             held = stage.tile([P, planes, H], F32, name=f"x_raw{a}{h}", offset=X_RAW_AT[a, h])
             x_raw[a, h] = held[:, 0:4, :]
-            rows = x[512 * a : 512 * (a + 1), h * H : (h + 1) * H]
-            nc.sync.dma_start(x_raw[a, h], rows.rearrange("(p i) j -> p i j", i=4))
+            x_rows = x[512 * a : 512 * (a + 1), h * H : (h + 1) * H]
+            nc.sync.dma_start(x_raw[a, h], x_rows.rearrange("(p i) j -> p i j", i=4))
 
-        load_x(0, 0)
-        load_x(1, 0, planes=16)
+        load_scales(nc.gpsimd, w_scales, w_sc, range(2, 4))
         for g, iw in enumerate((iw0, iw1, iw2, iw3)):
             nc.gpsimd.dma_start(
                 iw_rows[g:P:32, :].rearrange("q (c m) -> q c m", m=32), iw.rearrange("(c q m) -> q c m", q=4, m=32)
             )
-        wx_c = keep.tile([P, PASSES, N], I32, name="wx_c", align_bytes=64)
-        nc.sync.dma_start(wx_c[:], wx_words.rearrange("a p n i -> p a (n i)").bitcast(I32))
         load_scales(nc.gpsimd, wx_scales, wx_sc, range(4))
-
-        ones = keep.tile([P, P], F32, name="ones")
-        nc.vector.memset(ones[:], 1.0)
-        ident = keep.tile([P, P], F32, name="ident")
-        nc.scalar.activation(ident[:], ones[:], COPY, scale=0.0)
-        count = keep.tile([P, P], F32, name="count", align_bytes=64)
-        nc.vector.tensor_tensor_scan(count[:], ones[:], ones[:], 0.0, MULT, ADD)
-        count_t = keep.tile([P, P], F32, name="count_t", align_bytes=64)
-        nc.vector.transpose(count_t[:], count[:])
-        for q in range(4):
-            blk = slice(32 * q, 32 * (q + 1))
-            nc.vector.tensor_tensor(ident[blk, blk], count[blk, blk], count_t[blk, blk], EQ)
 
         picked_sc = {}
         parted = {}
 
-        def gather_scales(g0, g1, gs, mover):
+        def gather_scales(g0, g1, gs, planes):
             nc.vector.tensor_copy(gs[:], tab_sc[:].bitcast(U8).indirect(offsets[:, 32 * g0 : 32 * g1]))
-            mover.dma_start(moved[0 : P - SHIFT, g0 * J // 4 : g1 * J // 4], gs[SHIFT:P, :].bitcast(I32))
             for g in range(g0, g1):
-                picked_sc[g] = gs[:, (g - g0) * J : (g - g0 + 1) * J]
+                picked_sc[g] = planes[:].bitcast(U8)[:, :, (g - g0) * J : (g - g0 + 1) * J]
+
+        def move_scales(gs, planes, a):
+            for r in range(4):
+                first = SC_AT + 16 * a + r
+                nc.sync.dma_start(planes[r:P:32, a, :], gs[first : first + 13 : 4, :].bitcast(I32))
 
         def gather_words(g, gw):
             nc.vector.tensor_copy(gw[:], tab_w[:].bitcast(U32).indirect(offsets[:, 32 * g : 32 * (g + 1)]))
@@ -127,19 +120,17 @@ def tile_list_interp_none_kernel(
                 nc.vector.tensor_copy(pt[:].bitcast(U16), src)
             parted[g] = pt
 
-        def table_pass(acc, g, jt, a):
-            if a == 0:
-                plane = picked_sc[g][:, jt * P : (jt + 1) * P]
-            else:
-                plane = moved[:].bitcast(U8)[:, g * J + jt * P : g * J + (jt + 1) * P]
+        def table_pass(acc, g, jt, step):
+            a = step if g == 0 else PASSES - 1 - step
+            plane = picked_sc[g][:, a, jt * P : (jt + 1) * P]
             nc.tensor.matmul_mx(
                 out=acc[:],
                 lhsT=parted[g][:, a, 2 * jt * P : 2 * (jt + 1) * P].bitcast(FP4X4),
                 lhsT_scale=plane,
                 rhs=w_c[:, a, :].bitcast(FP8X4),
                 rhs_scale=w_sc[:, a, :].bitcast(U8),
-                start=(a == 0),
-                stop=(a == PASSES - 1),
+                start=(step == 0),
+                stop=(step == PASSES - 1),
             )
 
         def bank(number):
@@ -155,16 +146,27 @@ def tile_list_interp_none_kernel(
         def weight(g, jt):
             return iw_col[:, 32 * jt + g : 32 * jt + g + 1]
 
-        gather_scales(0, 3, keep.tile([P, 3 * J], U8, name="picked_sc012", align_bytes=64), nc.scalar)
+        picked_sc01 = keep.tile([P, 2 * J], U8, name="picked_sc01", align_bytes=64)
+        picked_sc23 = keep.tile([P, 2 * J], U8, name="picked_sc23", align_bytes=64)
+        gather_scales(0, 2, picked_sc01, planes01)
+        gather_scales(2, 4, picked_sc23, planes23)
+        nc.sync.dma_start(w_c[:], w_words.rearrange("a p n i -> p a (n i)").bitcast(I32))
+        load_scales(nc.sync, w_scales, w_sc, range(2))
+        move_scales(picked_sc01, planes01, 0)
+        load_x(0, 0)
+        move_scales(picked_sc01, planes01, 1)
+        load_x(1, 0, planes=16)
+        nc.sync.dma_start(wx_c[:], wx_words.rearrange("a p n i -> p a (n i)").bitcast(I32))
+        for a in range(PASSES):
+            move_scales(picked_sc23, planes23, a)
+        load_x(0, 1)
+        load_x(1, 1)
         part(0, gather_words(0, reuse.tile([P, J], U32, name="picked_w0", align_bytes=64, offset=2048)))
-        iw_col = reuse.tile([P, P], F32, name="iw_col", align_bytes=64, offset=2560)
         picked_w1 = gather_words(1, reuse.tile([P, J], U32, name="picked_w1", align_bytes=64, offset=512))
-        nc.vector.transpose(iw_col[:], iw_rows[:])
         part(1, picked_w1)
         picked_w2 = gather_words(2, reuse.tile([P, J], U32, name="picked_w2", align_bytes=64, offset=3584))
-        load_x(0, 1)
-        gather_scales(3, 4, reuse.tile([P, J], U8, name="picked_sc3", align_bytes=64, offset=3072), nc.sync)
-        load_x(1, 1)
+        iw_col = reuse.tile([P, P], F32, name="iw_col", align_bytes=64, offset=2048)
+        nc.vector.transpose(iw_col[:], iw_rows[:])
         part(2, picked_w2)
 
         x_c = keep.tile([P, PASSES, J], U32, name="x_c", align_bytes=64)
@@ -181,8 +183,8 @@ def tile_list_interp_none_kernel(
                     x_raw[a, h].rearrange("p t (c i) -> p c t i", i=4),
                 )
 
-        def quantize_x(h):
-            for a in range(PASSES):
+        def quantize_x(h, passes=range(PASSES)):
+            for a in passes:
                 nc.vector.quantize_mx(
                     out=x_c[:, a, h * H : (h + 1) * H].bitcast(FP8X4),
                     scales=x_sc[:, a, h * H : (h + 1) * H],
@@ -244,40 +246,46 @@ def tile_list_interp_none_kernel(
         def held_tile(name, slot):
             return late.tile([P, N], F32, name=name, offset=X_BF_AT[0, 1][0] + 2048 * slot)
 
-        acc2 = table_products(2, range(JT), 0)
-        with_x, with2, with3, acc3, accx = {}, {}, {}, {}, {}
+        with_x, with2, with3, with12, acc3, accx = {}, {}, {}, {}, {}, {}
 
         def add_x(jt, acc, term, dst, cols=slice(0, N)):
             nc.vector.tensor_tensor(dst[:, cols], acc[:, cols], term[:, cols], ADD)
             return dst
 
+        def fresh(name):
+            return keep.tile([P, N], F32, name=name)
+
+        def add_1(jt, dst):
+            nc.gpsimd.tensor_tensor(dst[:], with2[jt][:], scaled[1, jt][:], ADD)
+            with12[jt] = dst
+
+        for jt in range(JT):
+            acc = table_products(2, [jt], jt)[jt]
+            with2[jt] = weigh_and_add(2, jt, acc, scaled[0, jt], fresh(f"with2_{jt}"))
+        add_1(0, fresh("with12_0"))
+        add_1(1, fresh("with12_1"))
         for jt in (0, 1):
             acc3[jt] = table_products(3, [jt], JT + jt)[jt]
-            with2[jt] = weigh_and_add(2, jt, acc2[jt], scaled[0, jt], keep.tile([P, N], F32, name=f"with2_{jt}"))
-        for jt in (0, 1):
-            accx[jt] = x_product(jt, jt)
-            if jt == 0:
-                acc3[2] = table_products(3, [2], JT + 2)[2]
-        for jt in (0, 1):
-            with3[jt] = weigh_and_add(3, jt, acc3[jt], scaled[1, jt], keep.tile([P, N], F32, name=f"with3_{jt}"))
-            with_x[jt] = add_x(jt, accx[jt], with2[jt], keep.tile([P, N], F32, name=f"with_x{jt}"))
-            turn_and_store(jt, (with3[jt], with_x[jt]), range(NT), nc.scalar.copy, JT + jt)
-            if jt == 0:
-                acc3[3] = table_products(3, [3], JT + 3)[3]
-        quantize_x(1)
-        for jt in (2, 3):
-            if jt == 2:
-                with2[jt] = weigh_and_add(2, jt, acc2[jt], scaled[1, jt], held_tile("with2_2", 0))
-            else:
-                with2[jt] = keep.tile([P, N], F32, name=f"with2_{jt}")
-                nc.scalar.activation(with2[jt][:], acc2[jt][:], COPY, scale=weight(2, jt))
             accx[jt] = x_product(jt, jt)
         for jt in (2, 3):
-            with3[jt] = weigh_and_add(3, jt, acc3[jt], scaled[0, jt], held_tile(f"with3_{jt}", jt - 1))
-        with_x[2] = add_x(2, accx[2], with2[2], keep.tile([P, N], F32, name="with_x2"))
-        turn_and_store(2, (with3[2], with_x[2]), range(NT), nc.scalar.copy, 0)
-        with_x[3] = keep.tile([P, N], F32, name="with_x3")
+            acc3[jt] = table_products(3, [jt], JT + jt)[jt]
+        with3[0] = weigh_and_add(3, 0, acc3[0], with12[0], fresh("with3_0"))
+        quantize_x(1, [0])
+        add_1(2, held_tile("with12_2", 0))
+        with3[1] = weigh_and_add(3, 1, acc3[1], with12[1], fresh("with3_1"))
+        with_x[0] = add_x(0, accx[0], with3[0], fresh("with_x0"))
+        quantize_x(1, [1])
+        turn_and_store(0, (with_x[0],), range(NT), nc.scalar.copy, JT)
+        with_x[1] = add_x(1, accx[1], with3[1], fresh("with_x1"))
+        for jt in (2, 3):
+            accx[jt] = x_product(jt, jt)
+        turn_and_store(1, (with_x[1],), range(NT), nc.scalar.copy, JT + 1)
+        with3[2] = weigh_and_add(3, 2, acc3[2], with12[2], fresh("with3_2"))
+        with3[3] = weigh_and_add(3, 3, acc3[3], with2[3], fresh("with3_3"))
+        with_x[2] = add_x(2, accx[2], with3[2], fresh("with_x2"))
+        turn_and_store(2, (with_x[2],), range(NT), nc.scalar.copy, JT + 2)
+        with_x[3] = fresh("with_x3")
         for half in range(2):
             add_x(3, accx[3], scaled[1, 3], with_x[3], slice(half * N // 2, (half + 1) * N // 2))
-        for blocks, copier, number in ((range(0, 2), nc.scalar.copy, 1), (range(2, 4), nc.vector.tensor_copy, 3)):
-            turn_and_store(3, (with2[3], with3[3], with_x[3]), blocks, copier, number)
+        for blocks, copier, number in ((range(0, 2), nc.scalar.copy, JT + 3), (range(2, 4), nc.vector.tensor_copy, 0)):
+            turn_and_store(3, (with3[3], with_x[3]), blocks, copier, number)

@@ -214,10 +214,12 @@ def tile_list_interp_none_kernel(
         for jt in range(JT):
             scaled[0, jt] = stage.tile([P, N], F32, name=f"scaled0_{jt}", offset=X_RAW_AT[1, 0] + 2048 * jt)
             nc.scalar.activation(scaled[0, jt][:], acc0[jt][:], COPY, scale=weight(0, jt))
+        acc1 = {}
         for jt in range(JT):
-            acc = table_products(1, [jt], JT + jt)[jt]
+            acc1[jt] = table_products(1, [jt], JT + jt)[jt]
+        for jt in range(JT - 1):
             scaled[1, jt] = stage.tile([P, N], F32, name=f"scaled1_{jt}", offset=X_RAW_AT[1, 0] + 2048 * (JT + jt))
-            nc.scalar.activation(scaled[1, jt][:], acc[:], COPY, scale=weight(1, jt))
+            nc.scalar.activation(scaled[1, jt][:], acc1[jt][:], COPY, scale=weight(1, jt))
         interleave_x(1)
 
         out_v = out.rearrange("(t p) j -> p t j", p=P)
@@ -243,10 +245,7 @@ def tile_list_interp_none_kernel(
             copier(res[:].rearrange("p t j -> p (t j)"), turn[:, : width * P])
             nc.sync.dma_start(out_v[:, blocks.start : blocks.stop, jt * P : (jt + 1) * P], res[:])
 
-        def held_tile(name, slot):
-            return late.tile([P, N], F32, name=name, offset=X_BF_AT[0, 1][0] + 2048 * slot)
-
-        with_x, with2, with3, with12, acc3, accx = {}, {}, {}, {}, {}, {}
+        with_x, with2, with3, acc3, accx = {}, {}, {}, {}, {}
 
         def add_x(jt, acc, term, dst, cols=slice(0, N)):
             nc.vector.tensor_tensor(dst[:, cols], acc[:, cols], term[:, cols], ADD)
@@ -255,37 +254,29 @@ def tile_list_interp_none_kernel(
         def fresh(name):
             return keep.tile([P, N], F32, name=name)
 
-        def add_1(jt, dst):
-            nc.gpsimd.tensor_tensor(dst[:], with2[jt][:], scaled[1, jt][:], ADD)
-            with12[jt] = dst
-
+        with1 = weigh_and_add(1, 3, acc1[3], scaled[0, 3], fresh("with1_3"))
         for jt in range(JT):
             acc = table_products(2, [jt], jt)[jt]
-            with2[jt] = weigh_and_add(2, jt, acc, scaled[0, jt], fresh(f"with2_{jt}"))
-        add_1(0, fresh("with12_0"))
-        add_1(1, fresh("with12_1"))
+            with2[jt] = weigh_and_add(2, jt, acc, scaled[0, jt] if jt < 3 else with1, fresh(f"with2_{jt}"))
         for jt in (0, 1):
             acc3[jt] = table_products(3, [jt], JT + jt)[jt]
             accx[jt] = x_product(jt, jt)
-        for jt in (2, 3):
-            acc3[jt] = table_products(3, [jt], JT + jt)[jt]
-        with3[0] = weigh_and_add(3, 0, acc3[0], with12[0], fresh("with3_0"))
-        quantize_x(1, [0])
-        add_1(2, held_tile("with12_2", 0))
-        with3[1] = weigh_and_add(3, 1, acc3[1], with12[1], fresh("with3_1"))
-        with_x[0] = add_x(0, accx[0], with3[0], fresh("with_x0"))
-        quantize_x(1, [1])
-        turn_and_store(0, (with_x[0],), range(NT), nc.scalar.copy, JT)
-        with_x[1] = add_x(1, accx[1], with3[1], fresh("with_x1"))
-        for jt in (2, 3):
-            accx[jt] = x_product(jt, jt)
-        turn_and_store(1, (with_x[1],), range(NT), nc.scalar.copy, JT + 1)
-        with3[2] = weigh_and_add(3, 2, acc3[2], with12[2], fresh("with3_2"))
+        acc3[2] = table_products(3, [2], JT + 2)[2]
+        for jt in (0, 1):
+            with3[jt] = weigh_and_add(3, jt, acc3[jt], scaled[1, jt], fresh(f"with3_{jt}"))
+            with_x[jt] = add_x(jt, accx[jt], with2[jt], fresh(f"with_x{jt}"))
+            turn_and_store(jt, (with3[jt], with_x[jt]), range(NT), nc.scalar.copy, JT + jt)
+            if jt == 0:
+                quantize_x(1)
+                acc3[3] = table_products(3, [3], JT + 3)[3]
+                accx[2] = x_product(2, 2)
+        accx[3] = x_product(3, 3)
+        with3[2] = weigh_and_add(3, 2, acc3[2], scaled[1, 2], fresh("with3_2"))
         with3[3] = weigh_and_add(3, 3, acc3[3], with2[3], fresh("with3_3"))
-        with_x[2] = add_x(2, accx[2], with3[2], fresh("with_x2"))
-        turn_and_store(2, (with_x[2],), range(NT), nc.scalar.copy, JT + 2)
+        with_x[2] = add_x(2, accx[2], with2[2], fresh("with_x2"))
+        turn_and_store(2, (with3[2], with_x[2]), range(NT), nc.scalar.copy, JT + 2)
         with_x[3] = fresh("with_x3")
         for half in range(2):
-            add_x(3, accx[3], scaled[1, 3], with_x[3], slice(half * N // 2, (half + 1) * N // 2))
+            add_x(3, accx[3], with3[3], with_x[3], slice(half * N // 2, (half + 1) * N // 2))
         for blocks, copier, number in ((range(0, 2), nc.scalar.copy, JT + 3), (range(2, 4), nc.vector.tensor_copy, 0)):
-            turn_and_store(3, (with3[3], with_x[3]), blocks, copier, number)
+            turn_and_store(3, (with_x[3],), blocks, copier, number)

@@ -43,16 +43,16 @@ def tile_list_interp_none_kernel(
         offsets = keep.tile([P, G * J // 16], U16, name="offsets")
 
         w_sc = keep.tile([P, PASSES, N // 4], I32, name="w_sc", align_bytes=64)
-        nc.gpsimd.memset(w_sc[:], 0)
+        nc.vector.memset(w_sc[:], 0)
         tab_sc = rows.tile([P, T // 4], I32, name="tab_sc", align_bytes=64, offset=0)
         nc.vector.memset(tab_sc[0:SC_AT, :], 0)
         planes01 = keep.tile([P, PASSES, 2 * J // 4], I32, name="planes01", align_bytes=64)
         nc.vector.memset(planes01[:], 0)
         wx_sc = keep.tile([P, PASSES, N // 4], I32, name="wx_sc", align_bytes=64)
+        nc.vector.memset(wx_sc[:], 0)
         planes23 = rows.tile([P, PASSES, 2 * J // 4], I32, name="planes23", align_bytes=64, offset=0)
-        iw_rows = late.tile([P, P], F32, name="iw_rows", align_bytes=64, offset=X_BF_AT[1, 1][0])
+        iw_rows = keep.tile([P, P], F32, name="iw_rows", align_bytes=64)
         nc.gpsimd.memset(iw_rows[:], 0.0)
-        nc.gpsimd.memset(wx_sc[:], 0)
         apart = keep.tile([P, P], F32, name="apart")
         nc.gpsimd.iota(apart[:], [[1, P]], base=0, channel_multiplier=-1, allow_small_or_imprecise_dtypes=True)
         distance = keep.tile([P, P], F32, name="distance")
@@ -83,7 +83,7 @@ def tile_list_interp_none_kernel(
             x_rows = x[512 * a : 512 * (a + 1), h * H : (h + 1) * H]
             nc.sync.dma_start(x_raw[a, h], x_rows.rearrange("(p i) j -> p i j", i=4))
 
-        load_scales(nc.gpsimd, w_scales, w_sc, range(2, 4))
+        load_scales(nc.gpsimd, w_scales, w_sc, range(2))
         for g, iw in enumerate((iw0, iw1, iw2, iw3)):
             nc.gpsimd.dma_start(
                 iw_rows[g:P:32, :].rearrange("q (c m) -> q c m", m=32), iw.rearrange("(c q m) -> q c m", q=4, m=32)
@@ -110,12 +110,17 @@ def tile_list_interp_none_kernel(
         def part(g, gw):
             if g in (1, 2):
                 pt = late.tile([P, PASSES, 2 * J], U8, name=f"parted{g}", align_bytes=64, offset=X_BF_AT[g - 1, 1][0])
+            elif g == 3:
+                pt = stage.tile([P, PASSES, 2 * J], U8, name=f"parted{g}", align_bytes=64, offset=X_RAW_AT[0, 0])
             else:
                 pt = keep.tile([P, PASSES, 2 * J], U8, name=f"parted{g}", align_bytes=64)
             src = gw[:].bitcast(U16).rearrange("p (j d) -> p d j", d=PASSES)
             if g == 0:
                 for a, cols in ((0, slice(0, P)), (0, slice(P, J)), (1, slice(0, J))):
                     nc.vector.tensor_copy(pt[:, a, :].bitcast(U16)[:, cols], src[:, a, cols])
+            elif g == 1:
+                for cols in (slice(0, P), slice(P, J)):
+                    nc.vector.tensor_copy(pt[:].bitcast(U16)[:, :, cols], src[:, :, cols])
             else:
                 nc.vector.tensor_copy(pt[:].bitcast(U16), src)
             parted[g] = pt
@@ -151,23 +156,24 @@ def tile_list_interp_none_kernel(
         gather_scales(0, 2, picked_sc01, planes01)
         gather_scales(2, 4, picked_sc23, planes23)
         nc.sync.dma_start(w_c[:], w_words.rearrange("a p n i -> p a (n i)").bitcast(I32))
-        load_scales(nc.sync, w_scales, w_sc, range(2))
+        load_scales(nc.sync, w_scales, w_sc, range(2, 4))
         move_scales(picked_sc01, planes01, 0)
         load_x(0, 0)
         move_scales(picked_sc01, planes01, 1)
         load_x(1, 0, planes=16)
-        nc.sync.dma_start(wx_c[:], wx_words.rearrange("a p n i -> p a (n i)").bitcast(I32))
         for a in range(PASSES):
             move_scales(picked_sc23, planes23, a)
+        nc.sync.dma_start(wx_c[:], wx_words.rearrange("a p n i -> p a (n i)").bitcast(I32))
         load_x(0, 1)
         load_x(1, 1)
         part(0, gather_words(0, reuse.tile([P, J], U32, name="picked_w0", align_bytes=64, offset=2048)))
-        picked_w1 = gather_words(1, reuse.tile([P, J], U32, name="picked_w1", align_bytes=64, offset=512))
-        part(1, picked_w1)
-        picked_w2 = gather_words(2, reuse.tile([P, J], U32, name="picked_w2", align_bytes=64, offset=3584))
-        iw_col = reuse.tile([P, P], F32, name="iw_col", align_bytes=64, offset=2048)
+        iw_col = reuse.tile([P, P], F32, name="iw_col", align_bytes=64, offset=2560)
         nc.vector.transpose(iw_col[:], iw_rows[:])
+        picked_w1 = gather_words(1, reuse.tile([P, J], U32, name="picked_w1", align_bytes=64, offset=512))
+        picked_w2 = gather_words(2, reuse.tile([P, J], U32, name="picked_w2", align_bytes=64, offset=3584))
+        part(1, picked_w1)
         part(2, picked_w2)
+        picked_w3 = gather_words(3, reuse.tile([P, J], U32, name="picked_w3", align_bytes=64, offset=0))
 
         x_c = keep.tile([P, PASSES, J], U32, name="x_c", align_bytes=64)
         x_sc = keep.tile([P, PASSES, J], U8, name="x_sc", align_bytes=64)
@@ -191,23 +197,25 @@ def tile_list_interp_none_kernel(
                     in_=x_bf[a, h].rearrange("p c t -> p (c t)"),
                 )
 
-        def x_product(jt, number):
+        def x_product(h, blocks, number):
             acc = bank(number)
-            for a in range(PASSES):
-                nc.tensor.matmul_mx(
-                    out=acc[:],
-                    lhsT=x_c[:, a, jt * P : (jt + 1) * P].bitcast(FP8X4),
-                    lhsT_scale=x_sc[:, a, jt * P : (jt + 1) * P],
-                    rhs=wx_c[:, a, :].bitcast(FP8X4),
-                    rhs_scale=wx_sc[:, a, :].bitcast(U8),
-                    start=(a == 0),
-                    stop=(a == PASSES - 1),
-                )
+            for i, nt in enumerate(blocks):
+                for a in range(PASSES):
+                    nc.tensor.matmul_mx(
+                        out=acc[:, i * H : (i + 1) * H],
+                        lhsT=wx_c[:, a, nt * P : (nt + 1) * P].bitcast(FP8X4),
+                        lhsT_scale=wx_sc[:, a, :].bitcast(U8)[:, nt * P : (nt + 1) * P],
+                        rhs=x_c[:, a, h * H : (h + 1) * H].bitcast(FP8X4),
+                        rhs_scale=x_sc[:, a, h * H : (h + 1) * H],
+                        start=(a == 0),
+                        stop=(a == PASSES - 1),
+                    )
             return acc
 
         interleave_x(0)
-        part(3, gather_words(3, reuse.tile([P, J], U32, name="picked_w3", align_bytes=64, offset=4096)))
-        quantize_x(0)
+        quantize_x(0, [0])
+        part(3, picked_w3)
+        quantize_x(0, [1])
 
         scaled = {}
         acc0 = table_products(0, range(JT), 0)
@@ -228,55 +236,57 @@ def tile_list_interp_none_kernel(
             nc.vector.scalar_tensor_tensor(dst[:], acc[:], weight(g, jt), term[:], MULT, ADD)
             return dst
 
-        def turn_and_store(jt, terms, blocks, copier, number):
+        turned = {}
+
+        def turn(h, pair, terms, number):
+            acc = bank(number)
+            steps = [(i, k, term) for i in range(2) for k in range(2) for term in terms[2 * h + k]]
+            for s, (i, k, term) in enumerate(steps):
+                nt = 2 * pair + i
+                nc.tensor.matmul(
+                    acc[:, i * H + k * P : i * H + (k + 1) * P],
+                    term[:, nt * P : (nt + 1) * P],
+                    ident[:],
+                    start=(s == 0),
+                    stop=(s == len(steps) - 1),
+                    is_transpose=True,
+                )
+            turned[h, pair] = keep.tile([P, N], F32, name=f"turned{h}{pair}")
+            nc.scalar.copy(turned[h, pair][:], acc[:])
+
+        def add_x_and_store(h, acc, blocks):
             width = len(blocks)
-            turn = bank(number)
-            for s, term in enumerate(terms):
-                for i, nt in enumerate(blocks):
-                    nc.tensor.matmul(
-                        turn[:, i * P : (i + 1) * P],
-                        term[:, nt * P : (nt + 1) * P],
-                        ident[:],
-                        start=(s == 0 and i == 0),
-                        stop=(s == len(terms) - 1 and i == width - 1),
-                        is_transpose=True,
-                    )
-            res = keep.tile([P, width, P], F32, name=f"res{jt}_{blocks.start}")
-            copier(res[:].rearrange("p t j -> p (t j)"), turn[:, : width * P])
-            nc.sync.dma_start(out_v[:, blocks.start : blocks.stop, jt * P : (jt + 1) * P], res[:])
-
-        with_x, with2, with3, acc3, accx = {}, {}, {}, {}, {}
-
-        def add_x(jt, acc, term, dst, cols=slice(0, N)):
-            nc.vector.tensor_tensor(dst[:, cols], acc[:, cols], term[:, cols], ADD)
-            return dst
+            at = (blocks.start % 2) * H
+            res = keep.tile([P, width, H], F32, name=f"res{h}_{blocks.start}")
+            nc.vector.tensor_tensor(
+                res[:].rearrange("p t j -> p (t j)"),
+                acc[:, : width * H],
+                turned[h, blocks.start // 2][:, at : at + width * H],
+                ADD,
+            )
+            nc.sync.dma_start(out_v[:, blocks.start : blocks.stop, h * H : (h + 1) * H], res[:])
 
         def fresh(name):
             return keep.tile([P, N], F32, name=name)
 
+        with2, with3, acc3, terms = {}, {}, {}, {}
         with1 = weigh_and_add(1, 3, acc1[3], scaled[0, 3], fresh("with1_3"))
         for jt in range(JT):
             acc = table_products(2, [jt], jt)[jt]
             with2[jt] = weigh_and_add(2, jt, acc, scaled[0, jt] if jt < 3 else with1, fresh(f"with2_{jt}"))
-        for jt in (0, 1):
+        for jt in range(JT):
             acc3[jt] = table_products(3, [jt], JT + jt)[jt]
-            accx[jt] = x_product(jt, jt)
-        acc3[2] = table_products(3, [2], JT + 2)[2]
-        for jt in (0, 1):
-            with3[jt] = weigh_and_add(3, jt, acc3[jt], scaled[1, jt], fresh(f"with3_{jt}"))
-            with_x[jt] = add_x(jt, accx[jt], with2[jt], fresh(f"with_x{jt}"))
-            turn_and_store(jt, (with3[jt], with_x[jt]), range(NT), nc.scalar.copy, JT + jt)
-            if jt == 0:
-                quantize_x(1)
-                acc3[3] = table_products(3, [3], JT + 3)[3]
-                accx[2] = x_product(2, 2)
-        accx[3] = x_product(3, 3)
-        with3[2] = weigh_and_add(3, 2, acc3[2], scaled[1, 2], fresh("with3_2"))
-        with3[3] = weigh_and_add(3, 3, acc3[3], with2[3], fresh("with3_3"))
-        with_x[2] = add_x(2, accx[2], with2[2], fresh("with_x2"))
-        turn_and_store(2, (with3[2], with_x[2]), range(NT), nc.scalar.copy, JT + 2)
-        with_x[3] = fresh("with_x3")
-        for half in range(2):
-            add_x(3, accx[3], with3[3], with_x[3], slice(half * N // 2, (half + 1) * N // 2))
-        for blocks, copier, number in ((range(0, 2), nc.scalar.copy, JT + 3), (range(2, 4), nc.vector.tensor_copy, 0)):
-            turn_and_store(3, (with_x[3],), blocks, copier, number)
+        pairs = [range(0, 2), range(2, 4)]
+        x_first = [x_product(0, blocks, pair) for pair, blocks in enumerate(pairs)]
+        for jt in range(JT):
+            with3[jt] = weigh_and_add(3, jt, acc3[jt], scaled[1, jt] if jt < 3 else with2[3], fresh(f"with3_{jt}"))
+            terms[jt] = (with2[jt], with3[jt]) if jt < 3 else (with3[jt],)
+        quantize_x(1)
+        for h in range(2):
+            for pair in range(2):
+                turn(h, pair, terms, 2 + 2 * h + pair)
+        x_second = [x_product(1, range(nt, nt + 1), (6, 7, 2, 3)[nt]) for nt in range(NT)]
+        for pair, blocks in enumerate(pairs):
+            add_x_and_store(0, x_first[pair], blocks)
+        for nt in range(NT):
+            add_x_and_store(1, x_second[nt], range(nt, nt + 1))

@@ -167,12 +167,12 @@ def tile_list_interp_none_kernel(
         load_x(0, 1)
         load_x(1, 1)
         part(0, gather_words(0, reuse.tile([P, J], U32, name="picked_w0", align_bytes=64, offset=2048)))
-        iw_col = reuse.tile([P, P], F32, name="iw_col", align_bytes=64, offset=2560)
-        nc.vector.transpose(iw_col[:], iw_rows[:])
         picked_w1 = gather_words(1, reuse.tile([P, J], U32, name="picked_w1", align_bytes=64, offset=512))
         picked_w2 = gather_words(2, reuse.tile([P, J], U32, name="picked_w2", align_bytes=64, offset=3584))
         part(1, picked_w1)
         part(2, picked_w2)
+        iw_col = reuse.tile([P, P], F32, name="iw_col", align_bytes=64, offset=2048)
+        nc.vector.transpose(iw_col[:], iw_rows[:])
         picked_w3 = gather_words(3, reuse.tile([P, J], U32, name="picked_w3", align_bytes=64, offset=0))
 
         x_c = keep.tile([P, PASSES, J], U32, name="x_c", align_bytes=64)
@@ -219,15 +219,11 @@ def tile_list_interp_none_kernel(
 
         scaled = {}
         acc0 = table_products(0, range(JT), 0)
-        for jt in range(JT):
-            scaled[0, jt] = stage.tile([P, N], F32, name=f"scaled0_{jt}", offset=X_RAW_AT[1, 0] + 2048 * jt)
-            nc.scalar.activation(scaled[0, jt][:], acc0[jt][:], COPY, scale=weight(0, jt))
-        acc1 = {}
-        for jt in range(JT):
-            acc1[jt] = table_products(1, [jt], JT + jt)[jt]
-        for jt in range(JT - 1):
-            scaled[1, jt] = stage.tile([P, N], F32, name=f"scaled1_{jt}", offset=X_RAW_AT[1, 0] + 2048 * (JT + jt))
-            nc.scalar.activation(scaled[1, jt][:], acc1[jt][:], COPY, scale=weight(1, jt))
+        acc1 = {jt: table_products(1, [jt], JT + jt)[jt] for jt in range(JT)}
+        for g, jt in ((0, 0), (0, 1), (1, 0), (1, 1), (0, 2), (0, 3), (1, 2)):
+            at = X_RAW_AT[1, 0] + 2048 * (JT * g + jt)
+            scaled[g, jt] = stage.tile([P, N], F32, name=f"scaled{g}_{jt}", offset=at)
+            nc.scalar.activation(scaled[g, jt][:], (acc0, acc1)[g][jt][:], COPY, scale=weight(g, jt))
         interleave_x(1)
 
         out_v = out.rearrange("(t p) j -> p t j", p=P)
@@ -269,23 +265,36 @@ def tile_list_interp_none_kernel(
         def fresh(name):
             return keep.tile([P, N], F32, name=name)
 
-        with2, with3, acc3, terms = {}, {}, {}, {}
-        with1 = weigh_and_add(1, 3, acc1[3], scaled[0, 3], fresh("with1_3"))
-        for jt in range(JT):
-            acc = table_products(2, [jt], jt)[jt]
-            with2[jt] = weigh_and_add(2, jt, acc, scaled[0, jt] if jt < 3 else with1, fresh(f"with2_{jt}"))
-        for jt in range(JT):
-            acc3[jt] = table_products(3, [jt], JT + jt)[jt]
+        acc2, acc3, terms = {}, {}, {}
         pairs = [range(0, 2), range(2, 4)]
-        x_first = [x_product(0, blocks, pair) for pair, blocks in enumerate(pairs)]
-        for jt in range(JT):
-            with3[jt] = weigh_and_add(3, jt, acc3[jt], scaled[1, jt] if jt < 3 else with2[3], fresh(f"with3_{jt}"))
-            terms[jt] = (with2[jt], with3[jt]) if jt < 3 else (with3[jt],)
+
+        def products(tiles):
+            for jt in tiles:
+                acc2[jt] = table_products(2, [jt], jt)[jt]
+            for jt in tiles:
+                acc3[jt] = table_products(3, [jt], JT + jt)[jt]
+
+        def weigh(g, jt, term):
+            return weigh_and_add(g, jt, (acc0, acc1, acc2, acc3)[g][jt], term, fresh(f"with{g}_{jt}"))
+
+        products(pairs[0])
+        with2 = {jt: weigh(2, jt, scaled[0, jt]) for jt in pairs[0]}
+        terms[0] = (with2[0], weigh(3, 0, scaled[1, 0]))
+        held = stage.tile([P, N], F32, name="with1_3", offset=X_RAW_AT[1, 0])
+        with1 = weigh_and_add(1, 3, acc1[3], scaled[0, 3], held)
+        terms[1] = (with2[1], weigh(3, 1, scaled[1, 1]))
+        products(pairs[1])
+        for pair in range(2):
+            turn(0, pair, terms, pair)
+        x_first = [x_product(0, blocks, JT + pair) for pair, blocks in enumerate(pairs)]
+        with2[2] = weigh(2, 2, scaled[0, 2])
+        with2[3] = weigh(2, 3, with1)
+        terms[2] = (with2[2], weigh(3, 2, scaled[1, 2]))
+        terms[3] = (weigh(3, 3, with2[3]),)
         quantize_x(1)
-        for h in range(2):
-            for pair in range(2):
-                turn(h, pair, terms, 2 + 2 * h + pair)
-        x_second = [x_product(1, range(nt, nt + 1), (6, 7, 2, 3)[nt]) for nt in range(NT)]
+        for pair in range(2):
+            turn(1, pair, terms, 2 + pair)
+        x_second = [x_product(1, range(nt, nt + 1), (6, 7, 0, 1)[nt]) for nt in range(NT)]
         for pair, blocks in enumerate(pairs):
             add_x_and_store(0, x_first[pair], blocks)
         for nt in range(NT):

@@ -51,7 +51,7 @@ def tile_list_interp_none_kernel(
         wx_sc = keep.tile([P, PASSES, N // 4], I32, name="wx_sc", align_bytes=64)
         nc.vector.memset(wx_sc[:], 0)
         planes23 = rows.tile([P, PASSES, 2 * J // 4], I32, name="planes23", align_bytes=64, offset=0)
-        iw_rows = keep.tile([P, P], F32, name="iw_rows", align_bytes=64)
+        iw_rows = reuse.tile([P, P], F32, name="iw_rows", align_bytes=64, offset=0)
         nc.gpsimd.memset(iw_rows[:], 0.0)
         apart = keep.tile([P, P], F32, name="apart")
         nc.gpsimd.iota(apart[:], [[1, P]], base=0, channel_multiplier=-1, allow_small_or_imprecise_dtypes=True)
@@ -84,12 +84,6 @@ def tile_list_interp_none_kernel(
             nc.sync.dma_start(x_raw[a, h], x_rows.rearrange("(p i) j -> p i j", i=4))
 
         load_scales(nc.gpsimd, w_scales, w_sc, range(2))
-        for g, iw in enumerate((iw0, iw1, iw2, iw3)):
-            nc.gpsimd.dma_start(
-                iw_rows[g:P:32, :].rearrange("q (c m) -> q c m", m=32), iw.rearrange("(c q m) -> q c m", q=4, m=32)
-            )
-        load_scales(nc.gpsimd, wx_scales, wx_sc, range(4))
-
         picked_sc = {}
         parted = {}
 
@@ -161,10 +155,15 @@ def tile_list_interp_none_kernel(
         load_x(0, 0)
         move_scales(picked_sc01, planes01, 1)
         load_x(1, 0, planes=16)
+        for g, iw in enumerate((iw0, iw1, iw2, iw3)):
+            nc.sync.dma_start(
+                iw_rows[g:P:32, :].rearrange("q (c m) -> q c m", m=32), iw.rearrange("(c q m) -> q c m", q=4, m=32)
+            )
         for a in range(PASSES):
             move_scales(picked_sc23, planes23, a)
         nc.sync.dma_start(wx_c[:], wx_words.rearrange("a p n i -> p a (n i)").bitcast(I32))
         load_x(0, 1)
+        load_scales(nc.sync, wx_scales, wx_sc, range(4))
         load_x(1, 1)
         part(0, gather_words(0, reuse.tile([P, J], U32, name="picked_w0", align_bytes=64, offset=2048)))
         picked_w1 = gather_words(1, reuse.tile([P, J], U32, name="picked_w1", align_bytes=64, offset=512))
@@ -220,7 +219,7 @@ def tile_list_interp_none_kernel(
         scaled = {}
         acc0 = table_products(0, range(JT), 0)
         acc1 = {jt: table_products(1, [jt], JT + jt)[jt] for jt in range(JT)}
-        for g, jt in ((0, 0), (0, 1), (1, 0), (1, 1), (0, 2), (0, 3), (1, 2)):
+        for g, jt in ((0, 0), (0, 1), (1, 0), (1, 1), (0, 2), (0, 3)):
             at = X_RAW_AT[1, 0] + 2048 * (JT * g + jt)
             scaled[g, jt] = stage.tile([P, N], F32, name=f"scaled{g}_{jt}", offset=at)
             nc.scalar.activation(scaled[g, jt][:], (acc0, acc1)[g][jt][:], COPY, scale=weight(g, jt))
@@ -279,18 +278,20 @@ def tile_list_interp_none_kernel(
 
         products(pairs[0])
         with2 = {jt: weigh(2, jt, scaled[0, jt]) for jt in pairs[0]}
-        terms[0] = (with2[0], weigh(3, 0, scaled[1, 0]))
-        held = stage.tile([P, N], F32, name="with1_3", offset=X_RAW_AT[1, 0])
-        with1 = weigh_and_add(1, 3, acc1[3], scaled[0, 3], held)
-        terms[1] = (with2[1], weigh(3, 1, scaled[1, 1]))
+        with1 = {}
+        for jt in pairs[1]:
+            held = stage.tile([P, N], F32, name=f"with1_{jt}", offset=X_RAW_AT[1, 0] + 2048 * (jt - 2))
+            with1[jt] = weigh_and_add(1, jt, acc1[jt], scaled[0, jt], held)
+        for jt in pairs[0]:
+            terms[jt] = (with2[jt], weigh(3, jt, scaled[1, jt]))
         products(pairs[1])
         for pair in range(2):
             turn(0, pair, terms, pair)
         x_first = [x_product(0, blocks, JT + pair) for pair, blocks in enumerate(pairs)]
-        with2[2] = weigh(2, 2, scaled[0, 2])
-        with2[3] = weigh(2, 3, with1)
-        terms[2] = (with2[2], weigh(3, 2, scaled[1, 2]))
-        terms[3] = (weigh(3, 3, with2[3]),)
+        for jt in pairs[1]:
+            with2[jt] = weigh(2, jt, with1[jt])
+        for jt in pairs[1]:
+            terms[jt] = (weigh(3, jt, with2[jt]),)
         quantize_x(1)
         for pair in range(2):
             turn(1, pair, terms, 2 + pair)

@@ -43,7 +43,7 @@ def tile_list_interp_none_kernel(
         offsets = keep.tile([P, G * J // 16], U16, name="offsets")
 
         w_sc = keep.tile([P, PASSES, N // 4], I32, name="w_sc", align_bytes=64)
-        nc.vector.memset(w_sc[:], 0)
+        nc.gpsimd.memset(w_sc[:], 0)
         tab_sc = rows.tile([P, T // 4], I32, name="tab_sc", align_bytes=64, offset=0)
         nc.vector.memset(tab_sc[0:SC_AT, :], 0)
         planes01 = keep.tile([P, PASSES, 2 * J // 4], I32, name="planes01", align_bytes=64)
@@ -51,8 +51,9 @@ def tile_list_interp_none_kernel(
         wx_sc = keep.tile([P, PASSES, N // 4], I32, name="wx_sc", align_bytes=64)
         nc.vector.memset(wx_sc[:], 0)
         planes23 = rows.tile([P, PASSES, 2 * J // 4], I32, name="planes23", align_bytes=64, offset=0)
-        iw_rows = reuse.tile([P, P], F32, name="iw_rows", align_bytes=64, offset=0)
-        nc.gpsimd.memset(iw_rows[:], 0.0)
+        iw_held = reuse.tile([P, 6 * P], F32, name="iw_rows", align_bytes=64, offset=5632)
+        iw_rows = iw_held[:, 0:P]
+        nc.gpsimd.memset(iw_rows, 0.0)
         apart = keep.tile([P, P], F32, name="apart")
         nc.gpsimd.iota(apart[:], [[1, P]], base=0, channel_multiplier=-1, allow_small_or_imprecise_dtypes=True)
         distance = keep.tile([P, P], F32, name="distance")
@@ -83,7 +84,7 @@ def tile_list_interp_none_kernel(
             x_rows = x[512 * a : 512 * (a + 1), h * H : (h + 1) * H]
             nc.sync.dma_start(x_raw[a, h], x_rows.rearrange("(p i) j -> p i j", i=4))
 
-        load_scales(nc.gpsimd, w_scales, w_sc, range(2))
+        load_scales(nc.scalar, w_scales, w_sc, range(2))
         picked_sc = {}
         parted = {}
 
@@ -157,7 +158,7 @@ def tile_list_interp_none_kernel(
         load_x(1, 0, planes=16)
         for g, iw in enumerate((iw0, iw1, iw2, iw3)):
             nc.sync.dma_start(
-                iw_rows[g:P:32, :].rearrange("q (c m) -> q c m", m=32), iw.rearrange("(c q m) -> q c m", q=4, m=32)
+                iw_held[g:P:32, 0:P].rearrange("q (c m) -> q c m", m=32), iw.rearrange("(c q m) -> q c m", q=4, m=32)
             )
         for a in range(PASSES):
             move_scales(picked_sc23, planes23, a)
@@ -171,11 +172,11 @@ def tile_list_interp_none_kernel(
         part(1, picked_w1)
         part(2, picked_w2)
         iw_col = reuse.tile([P, P], F32, name="iw_col", align_bytes=64, offset=2048)
-        nc.vector.transpose(iw_col[:], iw_rows[:])
-        picked_w3 = gather_words(3, reuse.tile([P, J], U32, name="picked_w3", align_bytes=64, offset=0))
+        nc.vector.transpose(iw_col[:], iw_rows)
+        picked_w3 = gather_words(3, reuse.tile([P, J], U32, name="picked_w3", align_bytes=64, offset=5632))
 
         x_c = keep.tile([P, PASSES, J], U32, name="x_c", align_bytes=64)
-        x_sc = keep.tile([P, PASSES, J], U8, name="x_sc", align_bytes=64)
+        x_sc = reuse.tile([P, PASSES, J], U8, name="x_sc", align_bytes=64, offset=5632 + 2048)
         x_bf = {}
 
         def interleave_x(h):

@@ -6,7 +6,7 @@ K, L, N, T, J = 1024, 1024, 512, 4096, 512
 G = 4
 P = 128
 PASSES = 2
-JT = J // P
+H = J // 2
 NT = N // P
 FLOPS = 2 * N * J * (G * K + L)
 
@@ -24,8 +24,7 @@ ABS = mybir.ActivationFunctionType.Abs
 RELU = mybir.ActivationFunctionType.Relu
 COPY = mybir.ActivationFunctionType.Copy
 SC_AT = 96
-X_RAW_AT = {(0, 0): 0, (1, 0): 4096, (0, 1): 20480, (1, 1): 24576}
-X_BF_AT = {(0, 0): (0, 2048), (1, 0): (2048, 2048), (0, 1): (4096, 2048), (1, 1): (6144, 10240)}
+SLOT = 4 * N
 
 
 def tile_list_interp_none_kernel(
@@ -34,35 +33,33 @@ def tile_list_interp_none_kernel(
     nc = tc.nc
     with ExitStack() as ctx:
         keep = ctx.enter_context(tc.tile_pool(name="keep", bufs=1))
-        reuse = ctx.enter_context(tc.tile_pool(name="reuse", bufs=1))
-        stage = ctx.enter_context(tc.tile_pool(name="stage", bufs=1))
-        late = ctx.enter_context(tc.tile_pool(name="late", bufs=1))
         rows = ctx.enter_context(tc.tile_pool(name="rows", bufs=1))
+        work = ctx.enter_context(tc.tile_pool(name="work", bufs=1))
         banks = ctx.enter_context(tc.psum_pool(name="banks", bufs=1))
+
+        def bank(number):
+            return banks.tile([P, N], F32, name=f"bank{number}", tag=f"bank{number}")
 
         offsets = keep.tile([P, G * J // 16], U16, name="offsets")
 
+        iw_held = work.tile([P, N], F32, name="iw_rows", align_bytes=64, offset=8 * SLOT)
+        iw_rows = iw_held[:, 0:32]
         w_sc = keep.tile([P, PASSES, N // 4], I32, name="w_sc", align_bytes=64)
         nc.gpsimd.memset(w_sc[:], 0)
-        tab_sc = rows.tile([P, T // 4], I32, name="tab_sc", align_bytes=64, offset=0)
-        nc.vector.memset(tab_sc[0:SC_AT, :], 0)
-        planes01 = keep.tile([P, PASSES, 2 * J // 4], I32, name="planes01", align_bytes=64)
-        nc.vector.memset(planes01[:], 0)
-        wx_sc = keep.tile([P, PASSES, N // 4], I32, name="wx_sc", align_bytes=64)
-        nc.vector.memset(wx_sc[:], 0)
-        planes23 = rows.tile([P, PASSES, 2 * J // 4], I32, name="planes23", align_bytes=64, offset=0)
-        iw_held = reuse.tile([P, 6 * P], F32, name="iw_rows", align_bytes=64, offset=5632)
-        iw_rows = iw_held[:, 0:P]
-        nc.gpsimd.memset(iw_rows, 0.0)
         apart = keep.tile([P, P], F32, name="apart")
         nc.gpsimd.iota(apart[:], [[1, P]], base=0, channel_multiplier=-1, allow_small_or_imprecise_dtypes=True)
-        distance = keep.tile([P, P], F32, name="distance")
-        nc.scalar.activation(distance[:], apart[:], ABS)
-        ident = keep.tile([P, P], F32, name="ident")
-        nc.scalar.activation(ident[:], distance[:], RELU, bias=1.0, scale=-1.0)
+        nc.gpsimd.memset(iw_rows, 0.0)
+        tab_sc = rows.tile([P, T // 4], I32, name="tab_sc", align_bytes=64, offset=0)
+        nc.vector.memset(tab_sc[0:SC_AT, :], 0)
+        early_plane = keep.tile([P, 2 * J // 4], I32, name="early_plane", align_bytes=64)
+        nc.vector.memset(early_plane[:], 0)
+        wx_sc = keep.tile([P, PASSES, N // 4], I32, name="wx_sc", align_bytes=64)
+        nc.vector.memset(wx_sc[:], 0)
+        pass1_plane = rows.tile([P, G * J // 4], I32, name="pass1_plane", align_bytes=64, offset=0)
+        late_plane = rows.tile([P, 2 * J // 4], I32, name="late_plane", align_bytes=64, offset=G * J)
 
-        def load_scales(engine, scales, plane, quadrants):
-            for q in quadrants:
+        def load_scales(engine, scales, plane):
+            for q in range(4):
                 engine.dma_start(
                     plane[32 * q : 32 * q + 4, :, :],
                     scales[:, 4 * q : 4 * q + 4, :].rearrange("a r n -> r a n").bitcast(I32),
@@ -72,137 +69,135 @@ def tile_list_interp_none_kernel(
         tab_rows = tab_words[0].rearrange("p t b -> p (t b)").bitcast(I32)
         nc.sync.dma_start(tab_sc[SC_AT:P, :], tab_scales.rearrange("a q t -> (a q) t").bitcast(I32))
         nc.sync.dma_start(offsets[:], offs)
-        nc.sync.dma_start(tab_w[:], tab_rows)
-        w_c = keep.tile([P, PASSES, N], I32, name="w_c", align_bytes=64)
+        nc.sync.dma_start(tab_w[:, 0 : T // 2], tab_rows[:, 0 : T // 2])
+        load_scales(nc.sync, w_scales, w_sc)
+        nc.sync.dma_start(tab_w[:, T // 2 : T], tab_rows[:, T // 2 : T])
+        distance = keep.tile([P, P], F32, name="distance")
+        nc.scalar.activation(distance[:], apart[:], ABS)
+        ident = keep.tile([P, P], F32, name="ident")
+        nc.scalar.activation(ident[:], distance[:], RELU, bias=1.0, scale=-1.0)
+        w_c = [keep.tile([P, N], I32, name=f"w_c{a}", align_bytes=64) for a in range(PASSES)]
         wx_c = keep.tile([P, PASSES, N], I32, name="wx_c", align_bytes=64)
-        H = J // 2
+        w_rows = w_words.rearrange("a p n i -> p a (n i)").bitcast(I32)
+        nc.sync.dma_start(w_c[0][:], w_rows[:, 0, :])
+        iw_col = keep.tile([P, 32], F32, name="iw_col", align_bytes=64)
+
+        def load_iw(g):
+            nc.sync.dma_start(iw_held[g:P:8, 0:32], (iw0, iw1, iw2, iw3)[g].rearrange("(c q m) -> q c m", q=4, m=32))
+
+        def weight(g, jt):
+            return iw_col[:, 8 * jt + g : 8 * jt + g + 1]
+
+        picked_sc = keep.tile([P, G * J // 4], I32, name="picked_sc", align_bytes=64)
+
+        def gather_scales(g0, g1):
+            nc.vector.tensor_copy(
+                picked_sc[:].bitcast(U8)[:, g0 * J : g1 * J], tab_sc[:].bitcast(U8).indirect(offsets[:, 32 * g0 : 32 * g1])
+            )
+
+        def move_scales(engine, plane, a, g0, g1):
+            for q in range(4):
+                first = SC_AT + 16 * a + 4 * q
+                engine.dma_start(plane[32 * q : 32 * q + 4, :], picked_sc[first : first + 4, g0 * J // 4 : g1 * J // 4])
+
+        def table_plane(g, a):
+            if a == 1:
+                return pass1_plane[:].bitcast(U8)[:, g * J : (g + 1) * J]
+            return (early_plane, late_plane)[g // 2][:].bitcast(U8)[:, (g % 2) * J : (g % 2 + 1) * J]
+
         x_raw = {}
 
-        def load_x(a, h, planes=4):
-            held = stage.tile([P, planes, H], F32, name=f"x_raw{a}{h}", offset=X_RAW_AT[a, h])
+        def load_x(a, h):
+            if (a, h) == (1, 0):
+                held = work.tile([P, 10, H], F32, name="x_raw10", offset=28 * SLOT)
+            else:
+                held = keep.tile([P, 4, H], F32, name=f"x_raw{a}{h}")
             x_raw[a, h] = held[:, 0:4, :]
             x_rows = x[512 * a : 512 * (a + 1), h * H : (h + 1) * H]
             nc.sync.dma_start(x_raw[a, h], x_rows.rearrange("(p i) j -> p i j", i=4))
 
-        load_scales(nc.scalar, w_scales, w_sc, range(2))
-        picked_sc = {}
+        gather_scales(0, 2)
+        gather_scales(2, 4)
+        move_scales(nc.sync, early_plane, 0, 0, 2)
+        nc.sync.dma_start(w_c[1][:], w_rows[:, 1, :])
+        for g in range(G):
+            load_iw(g)
+        move_scales(nc.sync, pass1_plane, 1, 0, 4)
+        load_x(0, 0)
+        load_x(1, 0)
+        nc.sync.dma_start(wx_c[:], wx_words.rearrange("a p n i -> p a (n i)").bitcast(I32))
+        load_scales(nc.sync, wx_scales, wx_sc)
+        move_scales(nc.sync, late_plane, 0, 2, 4)
+        load_x(0, 1)
+        load_x(1, 1)
+
+        picked_w = {}
         parted = {}
 
-        def gather_scales(g0, g1, gs, planes):
-            nc.vector.tensor_copy(gs[:], tab_sc[:].bitcast(U8).indirect(offsets[:, 32 * g0 : 32 * g1]))
-            for g in range(g0, g1):
-                picked_sc[g] = planes[:].bitcast(U8)[:, :, (g - g0) * J : (g - g0 + 1) * J]
+        def gather_words(g, h, at):
+            gw = work.tile([P, H], U32, name=f"picked_w{g}{h}", align_bytes=64, offset=at)
+            first = 32 * g + 16 * h
+            nc.vector.tensor_copy(gw[:], tab_w[:].bitcast(U32).indirect(offsets[:, first : first + 16]))
+            picked_w[g, h] = gw
 
-        def move_scales(gs, planes, a):
-            for r in range(4):
-                first = SC_AT + 16 * a + r
-                nc.sync.dma_start(planes[r:P:32, a, :], gs[first : first + 13 : 4, :].bitcast(I32))
-
-        def gather_words(g, gw):
-            nc.vector.tensor_copy(gw[:], tab_w[:].bitcast(U32).indirect(offsets[:, 32 * g : 32 * (g + 1)]))
-            return gw
-
-        def part(g, gw):
-            if g in (1, 2):
-                pt = late.tile([P, PASSES, 2 * J], U8, name=f"parted{g}", align_bytes=64, offset=X_BF_AT[g - 1, 1][0])
-            elif g == 3:
-                pt = stage.tile([P, PASSES, 2 * J], U8, name=f"parted{g}", align_bytes=64, offset=X_RAW_AT[0, 0])
+        def part(g, h):
+            src = picked_w[g, h][:].bitcast(U16).rearrange("p (j d) -> p d j", d=PASSES)
+            if (g, h) == (0, 0):
+                for a in range(PASSES):
+                    pt = keep.tile([P, 2 * H], U8, name=f"parted{g}{h}{a}", align_bytes=64)
+                    nc.vector.tensor_copy(pt[:].bitcast(U16), src[:, a, :])
+                    parted[g, h, a] = pt[:]
             else:
-                pt = keep.tile([P, PASSES, 2 * J], U8, name=f"parted{g}", align_bytes=64)
-            src = gw[:].bitcast(U16).rearrange("p (j d) -> p d j", d=PASSES)
-            if g == 0:
-                for a, cols in ((0, slice(0, P)), (0, slice(P, J)), (1, slice(0, J))):
-                    nc.vector.tensor_copy(pt[:, a, :].bitcast(U16)[:, cols], src[:, a, cols])
-            elif g == 1:
-                for cols in (slice(0, P), slice(P, J)):
-                    nc.vector.tensor_copy(pt[:].bitcast(U16)[:, :, cols], src[:, :, cols])
-            else:
+                pt = work.tile([P, PASSES, 2 * H], U8, name=f"parted{g}{h}", align_bytes=64, offset=(20 + 4 * h + g) * SLOT)
                 nc.vector.tensor_copy(pt[:].bitcast(U16), src)
-            parted[g] = pt
+                for a in range(PASSES):
+                    parted[g, h, a] = pt[:, a, :]
 
-        def table_pass(acc, g, jt, step):
-            a = step if g == 0 else PASSES - 1 - step
-            plane = picked_sc[g][:, a, jt * P : (jt + 1) * P]
+        acc = {}
+
+        def table_pass(g, jt, step):
+            h, i = divmod(jt, 2)
+            a = PASSES - 1 - step if g == 1 else step
             nc.tensor.matmul_mx(
-                out=acc[:],
-                lhsT=parted[g][:, a, 2 * jt * P : 2 * (jt + 1) * P].bitcast(FP4X4),
-                lhsT_scale=plane,
-                rhs=w_c[:, a, :].bitcast(FP8X4),
+                out=acc[g, jt][:],
+                lhsT=parted[g, h, a][:, 2 * i * P : 2 * (i + 1) * P].bitcast(FP4X4),
+                lhsT_scale=table_plane(g, a)[:, jt * P : (jt + 1) * P],
+                rhs=w_c[a][:].bitcast(FP8X4),
                 rhs_scale=w_sc[:, a, :].bitcast(U8),
                 start=(step == 0),
                 stop=(step == PASSES - 1),
             )
 
-        def bank(number):
-            return banks.tile([P, N], F32, name=f"bank{number}", tag=f"bank{number}")
-
-        def table_products(g, tiles, first_bank):
-            accs = {jt: bank(first_bank + i) for i, jt in enumerate(tiles)}
-            for a in range(PASSES):
-                for jt in tiles:
-                    table_pass(accs[jt], g, jt, a)
-            return accs
-
-        def weight(g, jt):
-            return iw_col[:, 32 * jt + g : 32 * jt + g + 1]
-
-        picked_sc01 = keep.tile([P, 2 * J], U8, name="picked_sc01", align_bytes=64)
-        picked_sc23 = keep.tile([P, 2 * J], U8, name="picked_sc23", align_bytes=64)
-        gather_scales(0, 2, picked_sc01, planes01)
-        gather_scales(2, 4, picked_sc23, planes23)
-        nc.sync.dma_start(w_c[:], w_words.rearrange("a p n i -> p a (n i)").bitcast(I32))
-        load_scales(nc.sync, w_scales, w_sc, range(2, 4))
-        move_scales(picked_sc01, planes01, 0)
-        load_x(0, 0)
-        move_scales(picked_sc01, planes01, 1)
-        load_x(1, 0, planes=16)
-        for g, iw in enumerate((iw0, iw1, iw2, iw3)):
-            nc.sync.dma_start(
-                iw_held[g:P:32, 0:P].rearrange("q (c m) -> q c m", m=32), iw.rearrange("(c q m) -> q c m", q=4, m=32)
-            )
-        for a in range(PASSES):
-            move_scales(picked_sc23, planes23, a)
-        nc.sync.dma_start(wx_c[:], wx_words.rearrange("a p n i -> p a (n i)").bitcast(I32))
-        load_x(0, 1)
-        load_scales(nc.sync, wx_scales, wx_sc, range(4))
-        load_x(1, 1)
-        part(0, gather_words(0, reuse.tile([P, J], U32, name="picked_w0", align_bytes=64, offset=2048)))
-        picked_w1 = gather_words(1, reuse.tile([P, J], U32, name="picked_w1", align_bytes=64, offset=512))
-        picked_w2 = gather_words(2, reuse.tile([P, J], U32, name="picked_w2", align_bytes=64, offset=3584))
-        part(1, picked_w1)
-        part(2, picked_w2)
-        iw_col = reuse.tile([P, P], F32, name="iw_col", align_bytes=64, offset=2048)
-        nc.vector.transpose(iw_col[:], iw_rows)
-        picked_w3 = gather_words(3, reuse.tile([P, J], U32, name="picked_w3", align_bytes=64, offset=5632))
+        def table_products(g, h, numbers):
+            for jt in (2 * h, 2 * h + 1):
+                acc[g, jt] = bank(numbers[jt % 2])
+                for step in range(PASSES):
+                    table_pass(g, jt, step)
 
         x_c = keep.tile([P, PASSES, J], U32, name="x_c", align_bytes=64)
-        x_sc = reuse.tile([P, PASSES, J], U8, name="x_sc", align_bytes=64, offset=5632 + 2048)
+        x_sc = keep.tile([P, PASSES, J], U8, name="x_sc", align_bytes=64)
         x_bf = {}
 
-        def interleave_x(h):
-            for a in range(PASSES):
-                at, span = X_BF_AT[a, h]
-                held = late.tile([P, span // 8, 4], BF16, name=f"xb{a}{h}", align_bytes=64, offset=at)
-                x_bf[a, h] = held[:, 0:H, :]
-                nc.scalar.copy(
-                    x_bf[a, h].rearrange("p (c i) t -> p c t i", i=4),
-                    x_raw[a, h].rearrange("p t (c i) -> p c t i", i=4),
-                )
+        def interleave_x(a, h, at):
+            x_bf[a, h] = work.tile([P, H, 4], BF16, name=f"xb{a}{h}", align_bytes=64, offset=at)
+            nc.scalar.copy(
+                x_bf[a, h][:].rearrange("p (c i) t -> p c t i", i=4),
+                x_raw[a, h].rearrange("p t (c i) -> p c t i", i=4),
+            )
 
-        def quantize_x(h, passes=range(PASSES)):
-            for a in passes:
-                nc.vector.quantize_mx(
-                    out=x_c[:, a, h * H : (h + 1) * H].bitcast(FP8X4),
-                    scales=x_sc[:, a, h * H : (h + 1) * H],
-                    in_=x_bf[a, h].rearrange("p c t -> p (c t)"),
-                )
+        def quantize_x(a, h):
+            nc.vector.quantize_mx(
+                out=x_c[:, a, h * H : (h + 1) * H].bitcast(FP8X4),
+                scales=x_sc[:, a, h * H : (h + 1) * H],
+                in_=x_bf[a, h][:].rearrange("p c t -> p (c t)"),
+            )
 
         def x_product(h, blocks, number):
-            acc = bank(number)
+            xa = bank(number)
             for i, nt in enumerate(blocks):
                 for a in range(PASSES):
                     nc.tensor.matmul_mx(
-                        out=acc[:, i * H : (i + 1) * H],
+                        out=xa[:, i * H : (i + 1) * H],
                         lhsT=wx_c[:, a, nt * P : (nt + 1) * P].bitcast(FP8X4),
                         lhsT_scale=wx_sc[:, a, :].bitcast(U8)[:, nt * P : (nt + 1) * P],
                         rhs=x_c[:, a, h * H : (h + 1) * H].bitcast(FP8X4),
@@ -210,93 +205,101 @@ def tile_list_interp_none_kernel(
                         start=(a == 0),
                         stop=(a == PASSES - 1),
                     )
-            return acc
+            return xa
 
-        interleave_x(0)
-        quantize_x(0, [0])
-        part(3, picked_w3)
-        quantize_x(0, [1])
+        def weigh(g, jt, at):
+            term = work.tile([P, N], F32, name=f"scaled{g}_{jt}", offset=at)
+            nc.scalar.activation(term[:], acc[g, jt][:], COPY, scale=weight(g, jt))
+            return term
 
-        scaled = {}
-        acc0 = table_products(0, range(JT), 0)
-        acc1 = {jt: table_products(1, [jt], JT + jt)[jt] for jt in range(JT)}
-        for g, jt in ((0, 0), (0, 1), (1, 0), (1, 1), (0, 2), (0, 3)):
-            at = X_RAW_AT[1, 0] + 2048 * (JT * g + jt)
-            scaled[g, jt] = stage.tile([P, N], F32, name=f"scaled{g}_{jt}", offset=at)
-            nc.scalar.activation(scaled[g, jt][:], (acc0, acc1)[g][jt][:], COPY, scale=weight(g, jt))
-        interleave_x(1)
-
-        out_v = out.rearrange("(t p) j -> p t j", p=P)
-
-        def weigh_and_add(g, jt, acc, term, dst):
-            nc.vector.scalar_tensor_tensor(dst[:], acc[:], weight(g, jt), term[:], MULT, ADD)
+        def weigh_and_add(g, jt, term):
+            dst = keep.tile([P, N], F32, name=f"with{g}_{jt}")
+            nc.vector.scalar_tensor_tensor(dst[:], acc[g, jt][:], weight(g, jt), term[:], MULT, ADD)
             return dst
 
         turned = {}
 
-        def turn(h, pair, terms, number):
-            acc = bank(number)
-            steps = [(i, k, term) for i in range(2) for k in range(2) for term in terms[2 * h + k]]
-            for s, (i, k, term) in enumerate(steps):
-                nt = 2 * pair + i
-                nc.tensor.matmul(
-                    acc[:, i * H + k * P : i * H + (k + 1) * P],
-                    term[:, nt * P : (nt + 1) * P],
-                    ident[:],
-                    start=(s == 0),
-                    stop=(s == len(steps) - 1),
-                    is_transpose=True,
-                )
-            turned[h, pair] = keep.tile([P, N], F32, name=f"turned{h}{pair}")
-            nc.scalar.copy(turned[h, pair][:], acc[:])
+        def turn(h, runs, numbers):
+            held = [bank(number) for number in numbers]
+            total = 2 * sum(len(run) for run in runs)
+            seen = [0, 0]
+            for run in runs:
+                for pair in range(2):
+                    for k, term in run:
+                        for i in range(2):
+                            nt = 2 * pair + i
+                            seen[pair] = seen[pair] + 1
+                            nc.tensor.matmul(
+                                held[pair][:, i * H + k * P : i * H + (k + 1) * P],
+                                term[:, nt * P : (nt + 1) * P],
+                                ident[:],
+                                start=(seen[pair] == 1),
+                                stop=(seen[pair] == total),
+                                is_transpose=True,
+                            )
+            for pair in range(2):
+                turned[h, pair] = keep.tile([P, N], F32, name=f"turned{h}{pair}")
+                nc.scalar.copy(turned[h, pair][:], held[pair][:])
 
-        def add_x_and_store(h, acc, blocks):
+        out_v = out.rearrange("(t p) j -> p t j", p=P)
+
+        def add_x_and_store(h, xa, blocks):
             width = len(blocks)
             at = (blocks.start % 2) * H
             res = keep.tile([P, width, H], F32, name=f"res{h}_{blocks.start}")
             nc.vector.tensor_tensor(
                 res[:].rearrange("p t j -> p (t j)"),
-                acc[:, : width * H],
+                xa[:, : width * H],
                 turned[h, blocks.start // 2][:, at : at + width * H],
                 ADD,
             )
             nc.sync.dma_start(out_v[:, blocks.start : blocks.stop, h * H : (h + 1) * H], res[:])
 
-        def fresh(name):
-            return keep.tile([P, N], F32, name=name)
-
-        acc2, acc3, terms = {}, {}, {}
         pairs = [range(0, 2), range(2, 4)]
 
-        def products(tiles):
-            for jt in tiles:
-                acc2[jt] = table_products(2, [jt], jt)[jt]
-            for jt in tiles:
-                acc3[jt] = table_products(3, [jt], JT + jt)[jt]
+        for g in range(G):
+            if g == 2:
+                nc.vector.transpose(iw_col[:], iw_rows)
+            for h in range(2):
+                gather_words(g, h, at=(9 - g // 2) * SLOT + h * 4 * H)
+            for h in range(2):
+                part(g, h)
+        for a in range(PASSES):
+            interleave_x(a, 0, (4 + a) * SLOT)
+            quantize_x(a, 0)
 
-        def weigh(g, jt, term):
-            return weigh_and_add(g, jt, (acc0, acc1, acc2, acc3)[g][jt], term, fresh(f"with{g}_{jt}"))
-
-        products(pairs[0])
-        with2 = {jt: weigh(2, jt, scaled[0, jt]) for jt in pairs[0]}
-        with1 = {}
-        for jt in pairs[1]:
-            held = stage.tile([P, N], F32, name=f"with1_{jt}", offset=X_RAW_AT[1, 0] + 2048 * (jt - 2))
-            with1[jt] = weigh_and_add(1, jt, acc1[jt], scaled[0, jt], held)
-        for jt in pairs[0]:
-            terms[jt] = (with2[jt], weigh(3, jt, scaled[1, jt]))
-        products(pairs[1])
-        for pair in range(2):
-            turn(0, pair, terms, pair)
-        x_first = [x_product(0, blocks, JT + pair) for pair, blocks in enumerate(pairs)]
-        for jt in pairs[1]:
-            with2[jt] = weigh(2, jt, with1[jt])
-        for jt in pairs[1]:
-            terms[jt] = (weigh(3, jt, with2[jt]),)
-        quantize_x(1)
-        for pair in range(2):
-            turn(1, pair, terms, 2 + pair)
-        x_second = [x_product(1, range(nt, nt + 1), (6, 7, 0, 1)[nt]) for nt in range(NT)]
+        for jt in range(4):
+            acc[0, jt] = bank(jt)
+        for step in range(PASSES):
+            for jt in range(4):
+                table_pass(0, jt, step)
+        table_products(1, 0, (4, 5))
+        table_products(1, 1, (6, 7))
+        order = [(0, 0), (0, 2), (0, 3), (0, 1), (1, 1)]
+        scaled = {(g, jt): weigh(g, jt, SLOT * (28 + i)) for i, (g, jt) in enumerate(order)}
+        interleave_x(0, 1, 25 * SLOT)
+        interleave_x(1, 1, 22 * SLOT)
+        sums = {jt: weigh_and_add(1, jt, scaled[0, jt]) for jt in (0, 2, 3)}
+        sums[1] = scaled[0, 1]
+        table_products(2, 0, (0, 2))
+        table_products(3, 0, (3, 1))
+        table_products(2, 1, (4, 6))
+        table_products(3, 1, (7, 5))
+        for jt in range(2):
+            sums[jt] = weigh_and_add(2, jt, sums[jt])
+        beside = sums[1]
+        sums[1] = scaled[1, 1]
+        for jt in range(2):
+            sums[jt] = weigh_and_add(3, jt, sums[jt])
+        for g in range(2, G):
+            for jt in range(2, 4):
+                sums[jt] = weigh_and_add(g, jt, sums[jt])
+        turn(0, [[(1, beside), (0, sums[0]), (1, sums[1])]], (0, 2))
+        x_first = [x_product(0, blocks, (3, 1)[pair]) for pair, blocks in enumerate(pairs)]
+        for a in range(PASSES):
+            quantize_x(a, 1)
+        turn(1, [[(jt - 2, sums[jt]) for jt in range(2, 4)]], (4, 6))
+        x_second = [x_product(1, range(nt, nt + 1), (7, 5, 0, 2)[nt]) for nt in range(NT)]
         for pair, blocks in enumerate(pairs):
             add_x_and_store(0, x_first[pair], blocks)
         for nt in range(NT):

@@ -109,7 +109,7 @@ def tile_list_interp_none_kernel(
 
         def load_x(a, h):
             if (a, h) == (1, 0):
-                held = work.tile([P, 10, H], F32, name="x_raw10", offset=28 * SLOT)
+                held = work.tile([P, 12, H], F32, name="x_raw10", offset=28 * SLOT)
             else:
                 held = keep.tile([P, 4, H], F32, name=f"x_raw{a}{h}")
             x_raw[a, h] = held[:, 0:4, :]
@@ -120,47 +120,47 @@ def tile_list_interp_none_kernel(
         gather_scales(2, 4)
         move_scales(nc.sync, early_plane, 0, 0, 2)
         nc.sync.dma_start(w_c[1][:], w_rows[:, 1, :])
-        for g in range(G):
-            load_iw(g)
         move_scales(nc.sync, pass1_plane, 1, 0, 4)
         load_x(0, 0)
+        for g in range(G):
+            load_iw(g)
         load_x(1, 0)
         nc.sync.dma_start(wx_c[:], wx_words.rearrange("a p n i -> p a (n i)").bitcast(I32))
-        load_scales(nc.sync, wx_scales, wx_sc)
         move_scales(nc.sync, late_plane, 0, 2, 4)
+        load_scales(nc.sync, wx_scales, wx_sc)
         load_x(0, 1)
         load_x(1, 1)
 
         picked_w = {}
         parted = {}
 
-        def gather_words(g, h, at):
-            gw = work.tile([P, H], U32, name=f"picked_w{g}{h}", align_bytes=64, offset=at)
-            first = 32 * g + 16 * h
-            nc.vector.tensor_copy(gw[:], tab_w[:].bitcast(U32).indirect(offsets[:, first : first + 16]))
-            picked_w[g, h] = gw
+        def gather_words(g, places, at, span):
+            held = work.tile([P, span], U32, name=f"picked_w{g}_{places.start}", align_bytes=64, offset=at)
+            gw = held[:, 0 : len(places)]
+            listed = offsets[:, 32 * g + places.start // 16 : 32 * g + places.stop // 16]
+            nc.vector.tensor_copy(gw, tab_w[:].bitcast(U32).indirect(listed))
+            picked_w[g, places.start] = gw.bitcast(U16).rearrange("p (j d) -> p d j", d=PASSES)
 
-        def part(g, h):
-            src = picked_w[g, h][:].bitcast(U16).rearrange("p (j d) -> p d j", d=PASSES)
-            if (g, h) == (0, 0):
-                for a in range(PASSES):
-                    pt = keep.tile([P, 2 * H], U8, name=f"parted{g}{h}{a}", align_bytes=64)
-                    nc.vector.tensor_copy(pt[:].bitcast(U16), src[:, a, :])
-                    parted[g, h, a] = pt[:]
+        def part(g, places, passes):
+            name = f"parted{g}_{places.start}_{passes.start}"
+            shape = [P, len(passes), 2 * len(places)]
+            if g == 0:
+                pt = keep.tile(shape, U8, name=name, align_bytes=64)
             else:
-                pt = work.tile([P, PASSES, 2 * H], U8, name=f"parted{g}{h}", align_bytes=64, offset=(20 + 4 * h + g) * SLOT)
-                nc.vector.tensor_copy(pt[:].bitcast(U16), src)
-                for a in range(PASSES):
-                    parted[g, h, a] = pt[:, a, :]
+                pt = work.tile(shape, U8, name=name, align_bytes=64, offset=(20 + g) * SLOT)
+            nc.vector.tensor_copy(pt[:].bitcast(U16), picked_w[g, places.start][:, passes.start : passes.stop, :])
+            for a in passes:
+                for jt in range(places.start // P, places.stop // P):
+                    at = 2 * (jt * P - places.start)
+                    parted[g, jt, a] = pt[:, a - passes.start, at : at + 2 * P]
 
         acc = {}
 
         def table_pass(g, jt, step):
-            h, i = divmod(jt, 2)
             a = PASSES - 1 - step if g == 1 else step
             nc.tensor.matmul_mx(
                 out=acc[g, jt][:],
-                lhsT=parted[g, h, a][:, 2 * i * P : 2 * (i + 1) * P].bitcast(FP4X4),
+                lhsT=parted[g, jt, a].bitcast(FP4X4),
                 lhsT_scale=table_plane(g, a)[:, jt * P : (jt + 1) * P],
                 rhs=w_c[a][:].bitcast(FP8X4),
                 rhs_scale=w_sc[:, a, :].bitcast(U8),
@@ -217,8 +217,6 @@ def tile_list_interp_none_kernel(
             nc.vector.scalar_tensor_tensor(dst[:], acc[g, jt][:], weight(g, jt), term[:], MULT, ADD)
             return dst
 
-        turned = {}
-
         def turn(h, runs, numbers):
             held = [bank(number) for number in numbers]
             total = 2 * sum(len(run) for run in runs)
@@ -237,36 +235,41 @@ def tile_list_interp_none_kernel(
                                 stop=(seen[pair] == total),
                                 is_transpose=True,
                             )
-            for pair in range(2):
-                turned[h, pair] = keep.tile([P, N], F32, name=f"turned{h}{pair}")
-                nc.scalar.copy(turned[h, pair][:], held[pair][:])
+            return held
+
+        def copy_out(name, source):
+            copied = keep.tile([P, N], F32, name=name)
+            nc.scalar.copy(copied[:], source[:])
+            return copied
 
         out_v = out.rearrange("(t p) j -> p t j", p=P)
 
-        def add_x_and_store(h, xa, blocks):
-            width = len(blocks)
-            at = (blocks.start % 2) * H
-            res = keep.tile([P, width, H], F32, name=f"res{h}_{blocks.start}")
-            nc.vector.tensor_tensor(
-                res[:].rearrange("p t j -> p (t j)"),
-                xa[:, : width * H],
-                turned[h, blocks.start // 2][:, at : at + width * H],
-                ADD,
-            )
+        def add_and_store(h, blocks, in_bank, copied):
+            res = keep.tile([P, len(blocks), H], F32, name=f"res{h}_{blocks.start}")
+            nc.vector.tensor_tensor(res[:].rearrange("p t j -> p (t j)"), in_bank, copied, ADD)
             nc.sync.dma_start(out_v[:, blocks.start : blocks.stop, h * H : (h + 1) * H], res[:])
 
         pairs = [range(0, 2), range(2, 4)]
 
-        for g in range(G):
-            if g == 2:
-                nc.vector.transpose(iw_col[:], iw_rows)
-            for h in range(2):
-                gather_words(g, h, at=(9 - g // 2) * SLOT + h * 4 * H)
-            for h in range(2):
-                part(g, h)
-        for a in range(PASSES):
-            interleave_x(a, 0, (4 + a) * SLOT)
-            quantize_x(a, 0)
+        halves = [range(0, H), range(H, J)]
+        whole = range(J)
+        both = range(PASSES)
+        gather_words(0, halves[0], 9 * SLOT, 2 * J)
+        gather_words(0, halves[1], 11 * SLOT, H)
+        part(0, halves[0], range(0, 1))
+        part(0, halves[0], range(1, 2))
+        part(0, halves[1], both)
+        gather_words(1, whole, 9 * SLOT, J)
+        gather_words(2, whole, 10 * SLOT, J)
+        part(1, whole, both)
+        part(2, whole, both)
+        nc.vector.transpose(iw_col[:], iw_rows)
+        gather_words(3, whole, 8 * SLOT, J)
+        interleave_x(0, 0, 4 * SLOT)
+        quantize_x(0, 0)
+        part(3, whole, both)
+        interleave_x(1, 0, 5 * SLOT)
+        quantize_x(1, 0)
 
         for jt in range(4):
             acc[0, jt] = bank(jt)
@@ -275,32 +278,29 @@ def tile_list_interp_none_kernel(
                 table_pass(0, jt, step)
         table_products(1, 0, (4, 5))
         table_products(1, 1, (6, 7))
-        order = [(0, 0), (0, 2), (0, 3), (0, 1), (1, 1)]
+        order = [(0, 0), (0, 2), (0, 3), (0, 1), (1, 0), (1, 1)]
         scaled = {(g, jt): weigh(g, jt, SLOT * (28 + i)) for i, (g, jt) in enumerate(order)}
-        interleave_x(0, 1, 25 * SLOT)
-        interleave_x(1, 1, 22 * SLOT)
-        sums = {jt: weigh_and_add(1, jt, scaled[0, jt]) for jt in (0, 2, 3)}
-        sums[1] = scaled[0, 1]
+        interleave_x(0, 1, 21 * SLOT)
+        interleave_x(1, 1, 6 * SLOT)
+        sums = {jt: weigh_and_add(1, jt, scaled[0, jt]) for jt in range(2, 4)}
         table_products(2, 0, (0, 2))
         table_products(3, 0, (3, 1))
-        table_products(2, 1, (4, 6))
+        table_products(2, 1, (6, 4))
         table_products(3, 1, (7, 5))
-        for jt in range(2):
-            sums[jt] = weigh_and_add(2, jt, sums[jt])
-        beside = sums[1]
-        sums[1] = scaled[1, 1]
-        for jt in range(2):
-            sums[jt] = weigh_and_add(3, jt, sums[jt])
+        terms = [(jt, weigh_and_add(g, jt, scaled[g - 2, jt])) for g in range(2, G) for jt in range(2)]
         for g in range(2, G):
             for jt in range(2, 4):
                 sums[jt] = weigh_and_add(g, jt, sums[jt])
-        turn(0, [[(1, beside), (0, sums[0]), (1, sums[1])]], (0, 2))
+        turned_first = turn(0, [terms], (0, 2))
+        copied_first = [copy_out(f"turned0{pair}", turned_first[pair]) for pair in range(2)]
         x_first = [x_product(0, blocks, (3, 1)[pair]) for pair, blocks in enumerate(pairs)]
-        for a in range(PASSES):
-            quantize_x(a, 1)
-        turn(1, [[(jt - 2, sums[jt]) for jt in range(2, 4)]], (4, 6))
+        quantize_x(0, 1)
+        add_and_store(0, pairs[0], x_first[0][:], copied_first[0][:])
+        quantize_x(1, 1)
+        turned_second = turn(1, [[(jt - 2, sums[jt]) for jt in range(2, 4)]], (6, 4))
+        copied_second = [copy_out(f"turned1{pair}", turned_second[pair]) for pair in range(2)]
         x_second = [x_product(1, range(nt, nt + 1), (7, 5, 0, 2)[nt]) for nt in range(NT)]
-        for pair, blocks in enumerate(pairs):
-            add_x_and_store(0, x_first[pair], blocks)
+        add_and_store(0, pairs[1], x_first[1][:], copied_first[1][:])
         for nt in range(NT):
-            add_x_and_store(1, x_second[nt], range(nt, nt + 1))
+            at = (nt % 2) * H
+            add_and_store(1, range(nt, nt + 1), x_second[nt][:, 0:H], copied_second[nt // 2][:, at : at + H])

@@ -69,9 +69,8 @@ def tile_list_interp_none_kernel(
         tab_rows = tab_words[0].rearrange("p t b -> p (t b)").bitcast(I32)
         nc.sync.dma_start(tab_sc[SC_AT:P, :], tab_scales.rearrange("a q t -> (a q) t").bitcast(I32))
         nc.sync.dma_start(offsets[:], offs)
-        nc.sync.dma_start(tab_w[:, 0 : T // 2], tab_rows[:, 0 : T // 2])
+        nc.sync.dma_start(tab_w[:], tab_rows)
         load_scales(nc.sync, w_scales, w_sc)
-        nc.sync.dma_start(tab_w[:, T // 2 : T], tab_rows[:, T // 2 : T])
         distance = keep.tile([P, P], F32, name="distance")
         nc.scalar.activation(distance[:], apart[:], ABS)
         ident = keep.tile([P, P], F32, name="ident")

@@ -290,16 +290,16 @@ def tile_list_interp_none_kernel(
         for g in range(2, G):
             for jt in range(2, 4):
                 sums[jt] = weigh_and_add(g, jt, sums[jt])
-        turned_first = turn(0, [terms], (0, 2))
-        copied_first = [copy_out(f"turned0{pair}", turned_first[pair]) for pair in range(2)]
-        x_first = [x_product(0, blocks, (3, 1)[pair]) for pair, blocks in enumerate(pairs)]
-        quantize_x(0, 1)
-        add_and_store(0, pairs[0], x_first[0][:], copied_first[0][:])
-        quantize_x(1, 1)
+        x_first = [x_product(0, blocks, (0, 2)[pair]) for pair, blocks in enumerate(pairs)]
+        x_copied = [copy_out(f"x_first{pair}", x_first[pair]) for pair in range(2)]
+        turned_first = turn(0, [terms], (3, 1))
+        for a in range(PASSES):
+            quantize_x(a, 1)
         turned_second = turn(1, [[(jt - 2, sums[jt]) for jt in range(2, 4)]], (6, 4))
-        copied_second = [copy_out(f"turned1{pair}", turned_second[pair]) for pair in range(2)]
+        turned_copied = [copy_out(f"turned{pair}", turned_second[pair]) for pair in range(2)]
         x_second = [x_product(1, range(nt, nt + 1), (7, 5, 0, 2)[nt]) for nt in range(NT)]
-        add_and_store(0, pairs[1], x_first[1][:], copied_first[1][:])
+        for pair, blocks in enumerate(pairs):
+            add_and_store(0, blocks, turned_first[pair][:], x_copied[pair][:])
         for nt in range(NT):
             at = (nt % 2) * H
-            add_and_store(1, range(nt, nt + 1), x_second[nt][:, 0:H], copied_second[nt // 2][:, at : at + H])
+            add_and_store(1, range(nt, nt + 1), x_second[nt][:, 0:H], turned_copied[nt // 2][:, at : at + H])

from contextlib import ExitStack

import concourse.mybir as mybir

K, L, N, T, J = 1024, 1024, 512, 4096, 512
G = 4
P = 128
PASSES = 2
H = J // 2
NT = N // P
FLOPS = 2 * N * J * (G * K + L)

F32 = mybir.dt.float32
BF16 = mybir.dt.bfloat16
I32 = mybir.dt.int32
U32 = mybir.dt.uint32
U16 = mybir.dt.uint16
U8 = mybir.dt.uint8
FP8X4 = mybir.dt.float8_e4m3fn_x4
FP4X4 = mybir.dt.float4_e2m1fn_x4
MULT = mybir.AluOpType.mult
ADD = mybir.AluOpType.add
ABS = mybir.ActivationFunctionType.Abs
RELU = mybir.ActivationFunctionType.Relu
COPY = mybir.ActivationFunctionType.Copy
SC_AT = 96
SLOT = 4 * N


def tile_list_interp_none_kernel(
    tc, tab_words, tab_scales, w_words, w_scales, x, wx_words, wx_scales, iw0, iw1, iw2, iw3, offs, out
):
    nc = tc.nc
    with ExitStack() as ctx:
        keep = ctx.enter_context(tc.tile_pool(name="keep", bufs=1))
        rows = ctx.enter_context(tc.tile_pool(name="rows", bufs=1))
        work = ctx.enter_context(tc.tile_pool(name="work", bufs=1))
        banks = ctx.enter_context(tc.psum_pool(name="banks", bufs=1))

        def bank(number):
            return banks.tile([P, N], F32, name=f"bank{number}", tag=f"bank{number}")

        offsets = keep.tile([P, G * J // 16], U16, name="offsets")

        iw_held = work.tile([P, N], F32, name="iw_rows", align_bytes=64, offset=8 * SLOT)
        iw_rows = iw_held[:, 0:32]
        w_sc = keep.tile([P, PASSES, N // 4], I32, name="w_sc", align_bytes=64)
        nc.gpsimd.memset(w_sc[:], 0)
        apart = keep.tile([P, P], F32, name="apart")
        nc.gpsimd.iota(apart[:], [[1, P]], base=0, channel_multiplier=-1, allow_small_or_imprecise_dtypes=True)
        nc.gpsimd.memset(iw_rows, 0.0)
        tab_sc = rows.tile([P, T // 4], I32, name="tab_sc", align_bytes=64, offset=0)
        nc.vector.memset(tab_sc[0:SC_AT, :], 0)
        early_plane = keep.tile([P, 2 * J // 4], I32, name="early_plane", align_bytes=64)
        nc.vector.memset(early_plane[:], 0)
        wx_sc = keep.tile([P, PASSES, N // 4], I32, name="wx_sc", align_bytes=64)
        nc.vector.memset(wx_sc[:], 0)
        pass1_plane = rows.tile([P, G * J // 4], I32, name="pass1_plane", align_bytes=64, offset=0)
        late_plane = rows.tile([P, 2 * J // 4], I32, name="late_plane", align_bytes=64, offset=G * J)

        def load_scales(engine, scales, plane):
            for q in range(4):
                engine.dma_start(
                    plane[32 * q : 32 * q + 4, :, :],
                    scales[:, 4 * q : 4 * q + 4, :].rearrange("a r n -> r a n").bitcast(I32),
                )

        tab_w = keep.tile([P, T], I32, name="tab_w", align_bytes=64)
        tab_rows = tab_words[0].rearrange("p t b -> p (t b)").bitcast(I32)
        nc.sync.dma_start(tab_sc[SC_AT:P, :], tab_scales.rearrange("a q t -> (a q) t").bitcast(I32))
        nc.sync.dma_start(offsets[:], offs)
        nc.sync.dma_start(tab_w[:], tab_rows)
        load_scales(nc.sync, w_scales, w_sc)
        distance = keep.tile([P, P], F32, name="distance")
        nc.scalar.activation(distance[:], apart[:], ABS)
        ident = keep.tile([P, P], F32, name="ident")
        nc.scalar.activation(ident[:], distance[:], RELU, bias=1.0, scale=-1.0)
        w_c = [keep.tile([P, N], I32, name=f"w_c{a}", align_bytes=64) for a in range(PASSES)]
        wx_c = keep.tile([P, PASSES, N], I32, name="wx_c", align_bytes=64)
        w_rows = w_words.rearrange("a p n i -> p a (n i)").bitcast(I32)
        nc.sync.dma_start(w_c[0][:], w_rows[:, 0, :])
        iw_col = keep.tile([P, 32], F32, name="iw_col", align_bytes=64)

        def load_iw(g):
            nc.sync.dma_start(iw_held[g:P:8, 0:32], (iw0, iw1, iw2, iw3)[g].rearrange("(c q m) -> q c m", q=4, m=32))

        def weight(g, jt):
            return iw_col[:, 8 * jt + g : 8 * jt + g + 1]

        picked_sc = keep.tile([P, G * J // 4], I32, name="picked_sc", align_bytes=64)

        def gather_scales(g0, g1):
            nc.vector.tensor_copy(
                picked_sc[:].bitcast(U8)[:, g0 * J : g1 * J], tab_sc[:].bitcast(U8).indirect(offsets[:, 32 * g0 : 32 * g1])
            )

        def move_scales(engine, plane, a, g0, g1):
            for q in range(4):
                first = SC_AT + 16 * a + 4 * q
                engine.dma_start(plane[32 * q : 32 * q + 4, :], picked_sc[first : first + 4, g0 * J // 4 : g1 * J // 4])

        def table_plane(g, a):
            if a == 1:
                return pass1_plane[:].bitcast(U8)[:, g * J : (g + 1) * J]
            return (early_plane, late_plane)[g // 2][:].bitcast(U8)[:, (g % 2) * J : (g % 2 + 1) * J]

        x_raw = {}

        def load_x(a, h):
            if (a, h) == (1, 0):
                held = work.tile([P, 12, H], F32, name="x_raw10", offset=28 * SLOT)
            else:
                held = keep.tile([P, 4, H], F32, name=f"x_raw{a}{h}")
            x_raw[a, h] = held[:, 0:4, :]
            x_rows = x[512 * a : 512 * (a + 1), h * H : (h + 1) * H]
            nc.sync.dma_start(x_raw[a, h], x_rows.rearrange("(p i) j -> p i j", i=4))

        gather_scales(0, 2)
        gather_scales(2, 4)
        move_scales(nc.sync, early_plane, 0, 0, 2)
        nc.sync.dma_start(w_c[1][:], w_rows[:, 1, :])
        move_scales(nc.sync, pass1_plane, 1, 0, 4)
        load_x(0, 0)
        for g in range(G):
            load_iw(g)
        load_x(1, 0)
        nc.sync.dma_start(wx_c[:], wx_words.rearrange("a p n i -> p a (n i)").bitcast(I32))
        move_scales(nc.sync, late_plane, 0, 2, 4)
        load_scales(nc.sync, wx_scales, wx_sc)
        load_x(0, 1)
        load_x(1, 1)

        picked_w = {}
        parted = {}

        def gather_words(g, places, at, span):
            held = work.tile([P, span], U32, name=f"picked_w{g}_{places.start}", align_bytes=64, offset=at)
            gw = held[:, 0 : len(places)]
            listed = offsets[:, 32 * g + places.start // 16 : 32 * g + places.stop // 16]
            nc.vector.tensor_copy(gw, tab_w[:].bitcast(U32).indirect(listed))
            picked_w[g, places.start] = gw.bitcast(U16).rearrange("p (j d) -> p d j", d=PASSES)

        def part(g, places, passes):
            name = f"parted{g}_{places.start}_{passes.start}"
            shape = [P, len(passes), 2 * len(places)]
            if g == 0:
                pt = keep.tile(shape, U8, name=name, align_bytes=64)
            else:
                pt = work.tile(shape, U8, name=name, align_bytes=64, offset=(20 + g) * SLOT)
            nc.vector.tensor_copy(pt[:].bitcast(U16), picked_w[g, places.start][:, passes.start : passes.stop, :])
            for a in passes:
                for jt in range(places.start // P, places.stop // P):
                    at = 2 * (jt * P - places.start)
                    parted[g, jt, a] = pt[:, a - passes.start, at : at + 2 * P]

        acc = {}

        def table_pass(g, jt, step):
            a = PASSES - 1 - step if g == 1 else step
            nc.tensor.matmul_mx(
                out=acc[g, jt][:],
                lhsT=parted[g, jt, a].bitcast(FP4X4),
                lhsT_scale=table_plane(g, a)[:, jt * P : (jt + 1) * P],
                rhs=w_c[a][:].bitcast(FP8X4),
                rhs_scale=w_sc[:, a, :].bitcast(U8),
                start=(step == 0),
                stop=(step == PASSES - 1),
            )

        def table_products(g, h, numbers):
            for jt in (2 * h, 2 * h + 1):
                acc[g, jt] = bank(numbers[jt % 2])
                for step in range(PASSES):
                    table_pass(g, jt, step)

        x_c = keep.tile([P, PASSES, J], U32, name="x_c", align_bytes=64)
        x_sc = keep.tile([P, PASSES, J], U8, name="x_sc", align_bytes=64)
        x_bf = {}

        def interleave_x(a, h, at):
            x_bf[a, h] = work.tile([P, H, 4], BF16, name=f"xb{a}{h}", align_bytes=64, offset=at)
            nc.scalar.copy(
                x_bf[a, h][:].rearrange("p (c i) t -> p c t i", i=4),
                x_raw[a, h].rearrange("p t (c i) -> p c t i", i=4),
            )

        def quantize_x(a, h):
            nc.vector.quantize_mx(
                out=x_c[:, a, h * H : (h + 1) * H].bitcast(FP8X4),
                scales=x_sc[:, a, h * H : (h + 1) * H],
                in_=x_bf[a, h][:].rearrange("p c t -> p (c t)"),
            )

        def x_product(h, blocks, number):
            xa = bank(number)
            for i, nt in enumerate(blocks):
                for a in range(PASSES):
                    nc.tensor.matmul_mx(
                        out=xa[:, i * H : (i + 1) * H],
                        lhsT=wx_c[:, a, nt * P : (nt + 1) * P].bitcast(FP8X4),
                        lhsT_scale=wx_sc[:, a, :].bitcast(U8)[:, nt * P : (nt + 1) * P],
                        rhs=x_c[:, a, h * H : (h + 1) * H].bitcast(FP8X4),
                        rhs_scale=x_sc[:, a, h * H : (h + 1) * H],
                        start=(a == 0),
                        stop=(a == PASSES - 1),
                    )
            return xa

        def weigh(g, jt, at):
            term = work.tile([P, N], F32, name=f"scaled{g}_{jt}", offset=at)
            nc.scalar.activation(term[:], acc[g, jt][:], COPY, scale=weight(g, jt))
            return term

        def weigh_and_add(g, jt, term):
            dst = keep.tile([P, N], F32, name=f"with{g}_{jt}")
            nc.vector.scalar_tensor_tensor(dst[:], acc[g, jt][:], weight(g, jt), term[:], MULT, ADD)
            return dst

        def turn(h, runs, numbers):
            held = [bank(number) for number in numbers]
            total = 2 * sum(len(run) for run in runs)
            seen = [0, 0]
            for run in runs:
                for pair in range(2):
                    for k, term in run:
                        for i in range(2):
                            nt = 2 * pair + i
                            seen[pair] = seen[pair] + 1
                            nc.tensor.matmul(
                                held[pair][:, i * H + k * P : i * H + (k + 1) * P],
                                term[:, nt * P : (nt + 1) * P],
                                ident[:],
                                start=(seen[pair] == 1),
                                stop=(seen[pair] == total),
                                is_transpose=True,
                            )
            return held

        def copy_out(name, source):
            copied = keep.tile([P, N], F32, name=name)
            nc.scalar.copy(copied[:], source[:])
            return copied

        out_v = out.rearrange("(t p) j -> p t j", p=P)

        def add_and_store(h, blocks, in_bank, copied):
            res = keep.tile([P, len(blocks), H], F32, name=f"res{h}_{blocks.start}")
            nc.vector.tensor_tensor(res[:].rearrange("p t j -> p (t j)"), in_bank, copied, ADD)
            nc.sync.dma_start(out_v[:, blocks.start : blocks.stop, h * H : (h + 1) * H], res[:])

        pairs = [range(0, 2), range(2, 4)]

        halves = [range(0, H), range(H, J)]
        whole = range(J)
        both = range(PASSES)
        gather_words(0, halves[0], 9 * SLOT, 2 * J)
        gather_words(0, halves[1], 11 * SLOT, H)
        part(0, halves[0], range(0, 1))
        part(0, halves[0], range(1, 2))
        part(0, halves[1], both)
        gather_words(1, whole, 9 * SLOT, J)
        gather_words(2, whole, 10 * SLOT, J)
        part(1, whole, both)
        part(2, whole, both)
        nc.vector.transpose(iw_col[:], iw_rows)
        gather_words(3, whole, 8 * SLOT, J)
        interleave_x(0, 0, 4 * SLOT)
        quantize_x(0, 0)
        part(3, whole, both)
        interleave_x(1, 0, 5 * SLOT)
        quantize_x(1, 0)

        for jt in range(4):
            acc[0, jt] = bank(jt)
        for step in range(PASSES):
            for jt in range(4):
                table_pass(0, jt, step)
        table_products(1, 0, (4, 5))
        table_products(1, 1, (6, 7))
        order = [(0, 0), (0, 2), (0, 3), (0, 1), (1, 0), (1, 1)]
        scaled = {(g, jt): weigh(g, jt, SLOT * (28 + i)) for i, (g, jt) in enumerate(order)}
        interleave_x(0, 1, 21 * SLOT)
        interleave_x(1, 1, 6 * SLOT)
        sums = {jt: weigh_and_add(1, jt, scaled[0, jt]) for jt in range(2, 4)}
        table_products(2, 0, (0, 2))
        table_products(3, 0, (3, 1))
        table_products(2, 1, (6, 4))
        table_products(3, 1, (7, 5))
        terms = [(jt, weigh_and_add(g, jt, scaled[g - 2, jt])) for g in range(2, G) for jt in range(2)]
        for g in range(2, G):
            for jt in range(2, 4):
                sums[jt] = weigh_and_add(g, jt, sums[jt])
        x_first = [x_product(0, blocks, (0, 2)[pair]) for pair, blocks in enumerate(pairs)]
        x_copied = [copy_out(f"x_first{pair}", x_first[pair]) for pair in range(2)]
        turned_first = turn(0, [terms], (3, 1))
        for a in range(PASSES):
            quantize_x(a, 1)
        turned_second = turn(1, [[(jt - 2, sums[jt]) for jt in range(2, 4)]], (6, 4))
        turned_copied = [copy_out(f"turned{pair}", turned_second[pair]) for pair in range(2)]
        x_second = [x_product(1, range(nt, nt + 1), (7, 5, 0, 2)[nt]) for nt in range(NT)]
        for pair, blocks in enumerate(pairs):
            add_and_store(0, blocks, turned_first[pair][:], x_copied[pair][:])
        for nt in range(NT):
            at = (nt % 2) * H
            add_and_store(1, range(nt, nt + 1), x_second[nt][:, 0:H], turned_copied[nt // 2][:, at : at + H])
